import numpy as np
import ml_dtypes


def mxq(x, axis, fmt="e4m3"):
    dtype, down = {"e4m3": (ml_dtypes.float8_e4m3fn, 7), "e5m2": (ml_dtypes.float8_e5m2, 14)}[fmt]
    v = np.moveaxis(np.asarray(x, np.float32).astype(ml_dtypes.bfloat16).astype(np.float64), axis, -1)
    blocks = v.reshape(v.shape[:-1] + (-1, 32))
    amax = np.abs(blocks).max(-1, keepdims=True)
    byte = np.maximum(np.where(amax > 0, np.frexp(amax)[1] - 1 + 127, 0) - down, 1)
    scale = np.exp2(byte - 127.0)
    codes = (blocks / scale).astype(np.float32).astype(dtype).astype(np.float64)
    return np.moveaxis((codes * scale).reshape(v.shape), -1, axis)


WIDE = False


def mx_kscale(k):
    if not WIDE:
        return np.ones(k)
    levels = np.array([10, -10, 5, -5, 0])
    if k % 512:
        return np.exp2(np.random.permutation(np.resize(levels, k // 32))).repeat(32)
    a = np.empty((k // 512, 16))
    for p in range(k // 512):
        a[p, :8] = np.random.permutation(np.resize(levels, 8))
        for g in range(8):
            far = levels[np.abs(levels - a[p, g]) >= 10]
            a[p, g + 8] = far[np.random.randint(len(far))]
    return np.exp2(a.ravel()).repeat(32)


def f64(x):
    return np.asarray(x).astype(np.float64)


def striped(idx):
    return np.tile(idx.reshape(-1, 16).T, (8, 1)).astype(np.uint16)


def unstriped(offs):
    return offs[:16].T.reshape(-1).astype(np.int64)


def pack_weight(w):
    k, n = w.shape
    w = f64(np.asarray(w, np.float32).astype(ml_dtypes.bfloat16)).reshape(k // 32, 32, n)
    amax = np.abs(w).max(1)
    byte = np.clip(np.where(amax > 0, np.frexp(amax)[1] - 1 + 127 - 7, 1), 1, 254)
    scaled = (w * np.exp2(127.0 - byte)[:, None, :]).reshape(k, n).astype(np.float32)
    words = np.ascontiguousarray(scaled.reshape(k // 512, 128, 4, n).transpose(0, 1, 3, 2)).astype(ml_dtypes.float8_e4m3fn).view(np.uint8)
    return words, np.ascontiguousarray(byte.astype(np.uint8).reshape(k // 512, 16, n))


def unpack_weight(words, scales):
    g, p, n, _ = words.shape
    vals = np.ascontiguousarray(words).view(ml_dtypes.float8_e4m3fn).astype(np.float64) * np.repeat(np.exp2(scales.astype(np.float64) - 127.0), 8, axis=1)[..., None]
    return vals.transpose(0, 1, 3, 2).reshape(g * 512, n)


def silu(v):
    return v / (1.0 + np.exp(-np.maximum(v, -700.0)))


K, T, H, N, J, U = 1024, 512, 512, 256, 512, 1024


def setup_inputs():
    n = np.random.standard_normal
    s = mx_kscale(K)[:, None]
    u = mx_kscale(H)
    r = mx_kscale(J)[:, None]
    packed_xT = pack_weight(n((K, T)) * s)
    return {
        "x_words": packed_xT[0],
        "x_scales": packed_xT[1],
        "aT": (n((J, U)) * r).astype(np.float32),
        "w1": (n((K, H)) / np.sqrt(K) / s * u).astype(np.float32),
        "w3": (n((J, H)) / np.sqrt(J) / r).astype(np.float32),
        "w2": (n((H, N)) / np.sqrt(2 * H) / u[:, None]).astype(np.float32),
        "pos1": striped(np.random.permutation(T)),
        "pos2": striped(np.random.permutation(T)),
    }


def reference(x_words, x_scales, aT, w1, w3, w2, pos1, pos2):
    xq = unpack_weight(x_words, x_scales)
    h = silu(mxq(f64(w1), 0, "e4m3").T @ xq)
    f = mxq(f64(w3), 0, "e4m3").T @ mxq(f64(aT), 0, "e4m3")
    z = h[:, unstriped(pos1)] * f[:, :T] + h[:, unstriped(pos2)] * f[:, T:2 * T]
    return silu(mxq(f64(w2), 0, "e4m3").T @ mxq(z, 0, "e4m3"))

@@ -1,0 +1,177 @@
+from contextlib import ExitStack
+
+import concourse.mybir as mybir
+
+K, T, H, N, J, U = 1024, 512, 512, 256, 512, 1024
+FLOPS = 2 * (K * H * T + J * H * U + H * N * T)
+
+F32 = mybir.dt.float32
+BF16 = mybir.dt.bfloat16
+I32 = mybir.dt.int32
+U32 = mybir.dt.uint32
+U16 = mybir.dt.uint16
+U8 = mybir.dt.uint8
+FP8X4 = mybir.dt.float8_e4m3fn_x4
+SILU = mybir.ActivationFunctionType.Silu
+MULT = mybir.AluOpType.mult
+ADD = mybir.AluOpType.add
+
+P = 128
+PACK = 4
+PASS = P * PACK
+PIECE = 256
+
+
+def tile_picked_wdime_silu_l_kernel(tc, x_words, x_scales, aT, w1, w3, w2, pos1, pos2, out):
+    nc = tc.nc
+    with ExitStack() as ctx:
+        sb = ctx.enter_context(tc.tile_pool(name="sb", bufs=1))
+        ps = ctx.enter_context(tc.psum_pool(name="ps", bufs=1))
+
+        def cast(engine, dst, src):
+            if engine == "v":
+                nc.vector.tensor_copy(out=dst, in_=src)
+            else:
+                nc.scalar.copy(out=dst, in_=src)
+
+        def quantise(name, grouped, width):
+            codes = sb.tile([P, width], U32, name=name + "_codes", align_bytes=64)
+            scales = sb.tile([P, width], U8, name=name + "_scales", align_bytes=64)
+            nc.vector.quantize_mx(out=codes[:].bitcast(FP8X4), scales=scales[:], in_=grouped)
+            return codes, scales
+
+        def load_rows(name, rows):
+            width = rows.shape[1]
+            raw = sb.tile([P, PACK, width], F32, name=name + "_raw")
+            nc.sync.dma_start(out=raw[:], in_=rows.rearrange("(p j) c -> p j c", j=PACK))
+            return raw
+
+        def weight_planes(name, raw, engines):
+            src = raw[:].rearrange("p j (q t r) -> p t q j r", t=PACK, r=4)
+            grouped = []
+            for t in range(PACK):
+                g = sb.tile([P, P * PACK], BF16, name="%s_bf%d" % (name, t), align_bytes=64)
+                cast(engines[t], g[:].rearrange("p (q r j) -> p q j r", r=4, j=PACK), src[:, t])
+                grouped.append(g)
+            return [quantise("%s_%d" % (name, t), grouped[t][:], P) for t in range(PACK)]
+
+        def plain_cast(name, raw, width, engine, tag):
+            g = sb.tile([P, width * PACK], BF16, name=name + "_bf", tag=tag, align_bytes=64)
+            cast(engine, g[:].rearrange("p (c r j) -> p c j r", r=4, j=PACK), raw[:].rearrange("p j (c r) -> p c j r", r=4))
+            return g
+
+        warm = sb.tile([P, 1], F32, name="warm")
+        nc.gpsimd.memset(warm[:], 0.0)
+        warm2 = sb.tile([P, 1], F32, name="warm2")
+        nc.scalar.activation(warm2[:], warm[:], SILU)
+
+        xs = sb.tile([P, 2 * T], U8, name="xs", align_bytes=64)
+        nc.gpsimd.memset(xs[:].bitcast(I32), 0)
+
+        w3_raw = load_rows("w3", w3)
+        a_raw = {}
+        a_raw[0] = load_rows("a0", aT[:, 0:PIECE])
+        for q in range(4):
+            nc.sync.dma_start(
+                out=xs[32 * q : 32 * q + 4, :].bitcast(I32).rearrange("r (z c) -> r z c", z=2),
+                in_=x_scales[:, 4 * q : 4 * q + 4, :].bitcast(I32).rearrange("z r c -> r z c"),
+            )
+        w1_raw = [load_rows("w1_%d" % g, w1[g * PASS : (g + 1) * PASS, :]) for g in range(2)]
+        xw = []
+        for g in range(2):
+            words = sb.tile([P, T], U32, name="xw%d" % g, align_bytes=64)
+            nc.sync.dma_start(out=words[:].bitcast(I32), in_=x_words[g].rearrange("p c r -> p (c r)").bitcast(I32))
+            xw.append(words)
+        lists = []
+        for d, pos in enumerate((pos1, pos2)):
+            offsets = sb.tile([P, T // 16], U16, name="offsets%d" % d)
+            nc.sync.dma_start(offsets[:], pos)
+            lists.append(offsets)
+        for u in (2, 1, 3):
+            a_raw[u] = load_rows("a%d" % u, aT[:, u * PIECE : (u + 1) * PIECE])
+        w2_raw = sb.tile([P, PACK, N], F32, name="w2_raw")
+        w2_rows = w2.rearrange("(q t r) n -> r q t n", t=PACK, r=4)
+        for r in range(4):
+            nc.sync.dma_start(out=w2_raw[r:P:4], in_=w2_rows[r])
+
+        w3_q = weight_planes("w3", w3_raw, "vsvv")
+
+        def filters(u, a_q):
+            codes, scales = a_q
+            tiles = []
+            for half in range(2):
+                bank = ps.tile([P, 2, PIECE], F32, name="f_bank", tag="f%d" % ((2 * u + half) % 4))
+                for s in range(2):
+                    wc, wsc = w3_q[2 * half + s]
+                    nc.tensor.matmul_mx(out=bank[:, s, :], lhsT=wc[:].bitcast(FP8X4), lhsT_scale=wsc[:],
+                                        rhs=codes[:].bitcast(FP8X4), rhs_scale=scales[:], start=True, stop=True)
+                f_sb = sb.tile([P, 2 * PIECE], F32, name="f%d_%d" % (u, half))
+                nc.scalar.copy(out=f_sb[:], in_=bank[:].rearrange("p s v -> p (s v)"))
+                tiles.append(f_sb)
+            return tiles
+
+        a_bf0 = plain_cast("a0", a_raw[0], PIECE, "v", "a0_bf")
+        f = {0: filters(0, quantise("a0", a_bf0[:], PIECE))}
+
+        w1_q = [weight_planes("w1_0", w1_raw[0], "vsvv"), weight_planes("w1_1", w1_raw[1], "vsvv")]
+
+        h_banks = [ps.tile([P, T], F32, name="h_bank%d" % t, tag="h%d" % t) for t in range(PACK)]
+        h = []
+        for g in range(2):
+            for t in range(PACK):
+                wc, wsc = w1_q[g][t]
+                nc.tensor.matmul_mx(out=h_banks[t][:], lhsT=wc[:].bitcast(FP8X4), lhsT_scale=wsc[:],
+                                    rhs=xw[g][:].bitcast(FP8X4), rhs_scale=xs[:, g * T : (g + 1) * T],
+                                    start=(g == 0), stop=(g == 1))
+        for t in range(PACK):
+            ht = sb.tile([P, T], F32, name="h%d" % t)
+            nc.scalar.activation(ht[:], h_banks[t][:], SILU)
+            h.append(ht)
+
+        def gathers(u, lo, width, prod):
+            d, half = u // 2, u % 2
+            v0 = half * PIECE + lo
+            for t in range(PACK):
+                f_t = f[u][t // 2][:, (t % 2) * PIECE + lo : (t % 2) * PIECE + lo + width]
+                nc.vector.tensor_tensor(prod[:, t, :], h[t][:].indirect(lists[d][:, v0 // 16 : (v0 + width) // 16]), f_t, MULT)
+
+        def add(name, pa, pb, width, tag):
+            z = sb.tile([P, width * PACK], BF16, name=name, tag=tag, align_bytes=64)
+            nc.vector.tensor_tensor(z[:].rearrange("p (c r t) -> p c t r", r=4, t=PACK),
+                                    pa.rearrange("p t (c r) -> p c t r", r=4), pb.rearrange("p t (c r) -> p c t r", r=4), ADD)
+            return z
+
+        def project(name, z_q, v0, width, tag):
+            codes, scales = z_q
+            bank = ps.tile([P, 2, width], F32, name=name + "_bank", tag=tag)
+            for m in range(2):
+                nc.tensor.matmul_mx(out=bank[:, m, :], lhsT=w2_codes[:, m * P : (m + 1) * P].bitcast(FP8X4),
+                                    lhsT_scale=w2_scales[:, m * P : (m + 1) * P],
+                                    rhs=codes[:].bitcast(FP8X4), rhs_scale=scales[:], start=True, stop=True)
+            o = sb.tile([P, 2, width], F32, name=name + "_o")
+            nc.scalar.activation(o[:], bank[:], SILU)
+            nc.sync.dma_start(out=out.rearrange("(m p) v -> p m v", p=P)[:, :, v0 : v0 + width], in_=o[:])
+
+        a_bf2 = plain_cast("a2", a_raw[2], PIECE, "v", "a2_bf")
+        f[2] = filters(2, quantise("a2", a_bf2[:], PIECE))
+        a_bf1 = plain_cast("a1", a_raw[1], PIECE, "s", "a1_bf")
+        f[1] = filters(1, quantise("a1", a_bf1[:], PIECE))
+        a_bf3 = plain_cast("a3", a_raw[3], PIECE, "s", "a3_bf")
+        f[3] = filters(3, quantise("a3", a_bf3[:], PIECE))
+        w2_bf = plain_cast("w2", w2_raw, N, "s", "w2_bf")
+        w2_codes, w2_scales = quantise("w2", w2_bf[:], N)
+
+        p0 = sb.tile([P, PACK, PIECE], F32, name="p0")
+        gathers(0, 0, PIECE, p0)
+        p2 = sb.tile([P, PACK, PIECE], F32, name="p2")
+        gathers(2, 0, PIECE, p2)
+        za = add("za", p0[:], p2[:], PIECE, "a1_bf")
+        za_q = quantise("za", za[:], PIECE)
+        project("oa", za_q, 0, PIECE, "h0")
+        p1 = sb.tile([P, PACK, PIECE], F32, name="p1")
+        gathers(1, 0, PIECE, p1)
+        for s in range(2):
+            p3 = sb.tile([P, PACK, P], F32, name="p3_%d" % s)
+            gathers(3, s * P, P, p3)
+            zb = add("zb%d" % s, p1[:, :, s * P : (s + 1) * P], p3[:], P, "zb%d" % s)
+            project("ob%d" % s, quantise("zb%d" % s, zb[:], P), PIECE + s * P, P, "h%d" % (1 + s))

@@ -1,6 +1,7 @@
 from contextlib import ExitStack
 
 import concourse.mybir as mybir
+from concourse.masks import make_identity
 
 K, T, H, N, J, U = 1024, 512, 512, 256, 512, 1024
 FLOPS = 2 * (K * H * T + J * H * U + H * N * T)
@@ -48,12 +49,12 @@ def tile_picked_wdime_silu_l_kernel(tc, x_words, x_scales, aT, w1, w3, w2, pos1,
 
         def weight_planes(name, raw, engines):
             src = raw[:].rearrange("p j (q t r) -> p t q j r", t=PACK, r=4)
-            grouped = []
+            planes = []
             for t in range(PACK):
                 g = sb.tile([P, P * PACK], BF16, name="%s_bf%d" % (name, t), align_bytes=64)
                 cast(engines[t], g[:].rearrange("p (q r j) -> p q j r", r=4, j=PACK), src[:, t])
-                grouped.append(g)
-            return [quantise("%s_%d" % (name, t), grouped[t][:], P) for t in range(PACK)]
+                planes.append(quantise("%s_%d" % (name, t), g[:], P))
+            return planes
 
         def plain_cast(name, raw, width, engine, tag):
             g = sb.tile([P, width * PACK], BF16, name=name + "_bf", tag=tag, align_bytes=64)
@@ -61,84 +62,116 @@ def tile_picked_wdime_silu_l_kernel(tc, x_words, x_scales, aT, w1, w3, w2, pos1,
             return g
 
         warm = sb.tile([P, 1], F32, name="warm")
-        nc.gpsimd.memset(warm[:], 0.0)
+        nc.vector.memset(warm[:], 0.0)
         warm2 = sb.tile([P, 1], F32, name="warm2")
         nc.scalar.activation(warm2[:], warm[:], SILU)
 
         xs = sb.tile([P, 2 * T], U8, name="xs", align_bytes=64)
         nc.gpsimd.memset(xs[:].bitcast(I32), 0)
+        ident = sb.tile([P, P], F32, name="ident")
+        make_identity(nc, ident[:])
+
+        def load_words(g):
+            words = sb.tile([P, T], U32, name="xw%d" % g, align_bytes=64)
+            nc.sync.dma_start(out=words[:].bitcast(I32), in_=x_words[g].rearrange("p c r -> p (c r)").bitcast(I32))
+            return words
 
         w3_raw = load_rows("w3", w3)
-        a_raw = {}
-        a_raw[0] = load_rows("a0", aT[:, 0:PIECE])
+        a_raw = [load_rows("a0", aT[:, 0:PIECE])]
         for q in range(4):
             nc.sync.dma_start(
                 out=xs[32 * q : 32 * q + 4, :].bitcast(I32).rearrange("r (z c) -> r z c", z=2),
                 in_=x_scales[:, 4 * q : 4 * q + 4, :].bitcast(I32).rearrange("z r c -> r z c"),
             )
-        w1_raw = [load_rows("w1_%d" % g, w1[g * PASS : (g + 1) * PASS, :]) for g in range(2)]
-        xw = []
-        for g in range(2):
-            words = sb.tile([P, T], U32, name="xw%d" % g, align_bytes=64)
-            nc.sync.dma_start(out=words[:].bitcast(I32), in_=x_words[g].rearrange("p c r -> p (c r)").bitcast(I32))
-            xw.append(words)
+        w1_raw = [load_rows("w1_0", w1[0:PASS, :])]
+        xw = [load_words(0)]
+        w1_raw.append(load_rows("w1_1", w1[PASS : 2 * PASS, :]))
+        xw.append(load_words(1))
+        a_raw.append(load_rows("a1", aT[:, T : T + PIECE]))
         lists = []
         for d, pos in enumerate((pos1, pos2)):
             offsets = sb.tile([P, T // 16], U16, name="offsets%d" % d)
             nc.sync.dma_start(offsets[:], pos)
             lists.append(offsets)
-        for u in (2, 1, 3):
-            a_raw[u] = load_rows("a%d" % u, aT[:, u * PIECE : (u + 1) * PIECE])
+        a_raw += [load_rows("a%d" % (2 + d), aT[:, d * T + PIECE : (d + 1) * T]) for d in range(2)]
         w2_raw = sb.tile([P, PACK, N], F32, name="w2_raw")
         w2_rows = w2.rearrange("(q t r) n -> r q t n", t=PACK, r=4)
         for r in range(4):
             nc.sync.dma_start(out=w2_raw[r:P:4], in_=w2_rows[r])
 
-        w3_q = weight_planes("w3", w3_raw, "vsvv")
+        w3_bf = sb.tile([P, PACK * PASS], BF16, name="w3_bf", align_bytes=64)
+        w3_dst = w3_bf[:].rearrange("p (t q r j) -> p t q j r", t=PACK, r=4, j=PACK)
+        w3_src = w3_raw[:].rearrange("p j (q t r) -> p t q j r", t=PACK, r=4)
+        cast("v", w3_dst[:, 0:2], w3_src[:, 0:2])
+        cast("s", w3_dst[:, 2:4], w3_src[:, 2:4])
+        w3_codes, w3_scales = quantise("w3", w3_bf[:], H)
 
-        def filters(u, a_q):
-            codes, scales = a_q
-            tiles = []
+        def filters(u, engine, tags):
+            g = plain_cast("a%d" % u, a_raw[u], PIECE, engine, "a%d_bf" % u)
+            codes, scales = quantise("a%d" % u, g[:], PIECE)
+            banks = []
             for half in range(2):
-                bank = ps.tile([P, 2, PIECE], F32, name="f_bank", tag="f%d" % ((2 * u + half) % 4))
+                bank = ps.tile([P, 2 * PIECE], F32, name="f_bank", tag=tags[half])
                 for s in range(2):
-                    wc, wsc = w3_q[2 * half + s]
-                    nc.tensor.matmul_mx(out=bank[:, s, :], lhsT=wc[:].bitcast(FP8X4), lhsT_scale=wsc[:],
+                    cols = slice((2 * half + s) * P, (2 * half + s + 1) * P)
+                    nc.tensor.matmul_mx(out=bank[:, s * PIECE : (s + 1) * PIECE], lhsT=w3_codes[:, cols].bitcast(FP8X4), lhsT_scale=w3_scales[:, cols],
                                         rhs=codes[:].bitcast(FP8X4), rhs_scale=scales[:], start=True, stop=True)
-                f_sb = sb.tile([P, 2 * PIECE], F32, name="f%d_%d" % (u, half))
-                nc.scalar.copy(out=f_sb[:], in_=bank[:].rearrange("p s v -> p (s v)"))
-                tiles.append(f_sb)
-            return tiles
+                banks.append(bank)
+            return banks
 
-        a_bf0 = plain_cast("a0", a_raw[0], PIECE, "v", "a0_bf")
-        f = {0: filters(0, quantise("a0", a_bf0[:], PIECE))}
+        def to_sbuf(name, bank, tag=None):
+            f_sb = sb.tile([P, 2 * PIECE], F32, name=name, tag=tag or name)
+            nc.scalar.copy(out=f_sb[:], in_=bank[:])
+            return f_sb
 
-        w1_q = [weight_planes("w1_0", w1_raw[0], "vsvv"), weight_planes("w1_1", w1_raw[1], "vsvv")]
-
-        h_banks = [ps.tile([P, T], F32, name="h_bank%d" % t, tag="h%d" % t) for t in range(PACK)]
-        h = []
+        f0 = filters(0, "v", ("b4", "b5"))
+        f0_sb = [to_sbuf("f0_sb%d" % i, f0[i]) for i in range(2)]
+        h_banks = [ps.tile([P, T], F32, name="h_bank%d" % t, tag="b%d" % t) for t in range(PACK)]
+        w1_q = [weight_planes("w1_%d" % g, w1_raw[g], "vsvs") for g in range(2)]
         for g in range(2):
             for t in range(PACK):
                 wc, wsc = w1_q[g][t]
                 nc.tensor.matmul_mx(out=h_banks[t][:], lhsT=wc[:].bitcast(FP8X4), lhsT_scale=wsc[:],
                                     rhs=xw[g][:].bitcast(FP8X4), rhs_scale=xs[:, g * T : (g + 1) * T],
                                     start=(g == 0), stop=(g == 1))
+        h = []
         for t in range(PACK):
             ht = sb.tile([P, T], F32, name="h%d" % t)
             nc.scalar.activation(ht[:], h_banks[t][:], SILU)
             h.append(ht)
 
-        def gathers(u, lo, width, prod):
-            d, half = u // 2, u % 2
-            v0 = half * PIECE + lo
-            for t in range(PACK):
-                f_t = f[u][t // 2][:, (t % 2) * PIECE + lo : (t % 2) * PIECE + lo + width]
-                nc.vector.tensor_tensor(prod[:, t, :], h[t][:].indirect(lists[d][:, v0 // 16 : (v0 + width) // 16]), f_t, MULT)
+        def looked_up(t, d, v0, width):
+            return h[t][:].indirect(lists[d][:, v0 // 16 : (v0 + width) // 16])
 
-        def add(name, pa, pb, width, tag):
+        def times_bank(name, g, bank):
+            prod = sb.tile([P, 2 * PIECE], F32, name=name)
+            nc.vector.tensor_tensor(prod[:], g[:], bank[:], MULT)
+            return prod
+
+        def add_on_vector(name, pa, pb, width, tag):
             z = sb.tile([P, width * PACK], BF16, name=name, tag=tag, align_bytes=64)
             nc.vector.tensor_tensor(z[:].rearrange("p (c r t) -> p c t r", r=4, t=PACK),
                                     pa.rearrange("p t (c r) -> p c t r", r=4), pb.rearrange("p t (c r) -> p c t r", r=4), ADD)
+            return z
+
+        def add_on_tensor(name, terms, blocks, tags, back_tag, between):
+            back = ps.tile([P, blocks, 2, P], F32, name=name + "_back", tag=back_tag)
+            turned = []
+            for b in range(blocks):
+                bank = ps.tile([P, PACK, P], F32, name=name + "_sum", tag=tags[b])
+                for t in range(PACK):
+                    for d in range(2):
+                        nc.tensor.matmul(bank[:, t, :], lhsT=terms(t, d, b), rhs=ident[:], is_transpose=True, start=(d == 0), stop=(d == 1))
+                zt = sb.tile([P, PACK * P], BF16, name="%s_t%d" % (name, b))
+                nc.scalar.copy(out=zt[:].rearrange("v (u p e) -> v u p e", u=2, e=2), in_=bank[:].rearrange("v (u e) p -> v u p e", u=2))
+                turned.append(zt)
+            for b in range(blocks):
+                words = turned[b][:].bitcast(F32)
+                for u in range(2):
+                    nc.tensor.transpose(back[:, b, u, :], words[:, u * P : (u + 1) * P], ident[:])
+            between()
+            z = sb.tile([P, blocks * P * PACK], BF16, name=name, align_bytes=64)
+            nc.scalar.copy(out=z[:].bitcast(F32).rearrange("p (b v u) -> p b v u", b=blocks, u=2), in_=back[:].rearrange("p b u v -> p b v u"))
             return z
 
         def project(name, z_q, v0, width, tag):
@@ -152,26 +185,25 @@ def tile_picked_wdime_silu_l_kernel(tc, x_words, x_scales, aT, w1, w3, w2, pos1,
             nc.scalar.activation(o[:], bank[:], SILU)
             nc.sync.dma_start(out=out.rearrange("(m p) v -> p m v", p=P)[:, :, v0 : v0 + width], in_=o[:])
 
-        a_bf2 = plain_cast("a2", a_raw[2], PIECE, "v", "a2_bf")
-        f[2] = filters(2, quantise("a2", a_bf2[:], PIECE))
-        a_bf1 = plain_cast("a1", a_raw[1], PIECE, "s", "a1_bf")
-        f[1] = filters(1, quantise("a1", a_bf1[:], PIECE))
-        a_bf3 = plain_cast("a3", a_raw[3], PIECE, "s", "a3_bf")
-        f[3] = filters(3, quantise("a3", a_bf3[:], PIECE))
+        f1 = filters(1, "v", ("b6", "b7"))
+        f2 = filters(2, "s", ("b0", "b1"))
+        f1_sb = [to_sbuf("f1_sb%d" % i, f1[i], (None, "a2_raw")[i]) for i in range(2)]
+        f3 = filters(3, "s", ("b2", "b3"))
+        f2_sb = [to_sbuf("f2_sb%d" % i, f2[i]) for i in range(2)]
         w2_bf = plain_cast("w2", w2_raw, N, "s", "w2_bf")
         w2_codes, w2_scales = quantise("w2", w2_bf[:], N)
+        f3_sb = [to_sbuf("f3_sb0", f3[0])]
 
-        p0 = sb.tile([P, PACK, PIECE], F32, name="p0")
-        gathers(0, 0, PIECE, p0)
-        p2 = sb.tile([P, PACK, PIECE], F32, name="p2")
-        gathers(2, 0, PIECE, p2)
-        za = add("za", p0[:], p2[:], PIECE, "a1_bf")
-        za_q = quantise("za", za[:], PIECE)
-        project("oa", za_q, 0, PIECE, "h0")
-        p1 = sb.tile([P, PACK, PIECE], F32, name="p1")
-        gathers(1, 0, PIECE, p1)
+        def fused(name, f_sb, d, v0, tag):
+            prod = sb.tile([P, PACK, PIECE], F32, name=name, tag=tag, align_bytes=64)
+            for t in range(PACK):
+                nc.vector.tensor_tensor(prod[:, t, :], looked_up(t, d, v0, PIECE), f_sb[t // 2][:, (t % 2) * PIECE : (t % 2 + 1) * PIECE], MULT)
+            return prod
+
+        pa = [fused("pa0", f0_sb, 0, 0, "pa0"), fused("pa1", f1_sb, 1, 0, "pa1")]
+        za = add_on_tensor("za", lambda t, d, b: pa[d][:, t, b * P : (b + 1) * P], 2, ("b4", "b5"), "b6", lambda: f3_sb.append(to_sbuf("f3_sb1", f3[1], "za_t1")))
+        project("oa", quantise("za", za[:], PIECE), 0, PIECE, "b7")
+        pb = [fused("pb0", f2_sb, 0, PIECE, "pb0"), fused("pb1", f3_sb, 1, PIECE, "pb1")]
+        zb = [add_on_vector("zb%d" % s, pb[0][:, :, s * P : (s + 1) * P], pb[1][:, :, s * P : (s + 1) * P], P, ("zb0", "zb1")[s]) for s in range(2)]
         for s in range(2):
-            p3 = sb.tile([P, PACK, P], F32, name="p3_%d" % s)
-            gathers(3, s * P, P, p3)
-            zb = add("zb%d" % s, p1[:, :, s * P : (s + 1) * P], p3[:], P, "zb%d" % s)
-            project("ob%d" % s, quantise("zb%d" % s, zb[:], P), PIECE + s * P, P, "h%d" % (1 + s))
+            project("ob%d" % s, quantise("zb%d" % s, zb[s][:], P), PIECE + s * P, P, "b%d" % s)

@@ -76,35 +76,41 @@ def tile_picked_wdime_silu_l_kernel(tc, x_words, x_scales, aT, w1, w3, w2, pos1,
             nc.sync.dma_start(out=words[:].bitcast(I32), in_=x_words[g].rearrange("p c r -> p (c r)").bitcast(I32))
             return words
 
-        w3_raw = load_rows("w3", w3)
-        a_raw = [load_rows("a0", aT[:, 0:PIECE])]
+        w1_raw = [load_rows("w1_0", w1[0:PASS, :])]
         for q in range(4):
             nc.sync.dma_start(
                 out=xs[32 * q : 32 * q + 4, :].bitcast(I32).rearrange("r (z c) -> r z c", z=2),
                 in_=x_scales[:, 4 * q : 4 * q + 4, :].bitcast(I32).rearrange("z r c -> r z c"),
             )
-        w1_raw = [load_rows("w1_0", w1[0:PASS, :])]
         xw = [load_words(0)]
         w1_raw.append(load_rows("w1_1", w1[PASS : 2 * PASS, :]))
         xw.append(load_words(1))
-        a_raw.append(load_rows("a1", aT[:, T : T + PIECE]))
         lists = []
         for d, pos in enumerate((pos1, pos2)):
             offsets = sb.tile([P, T // 16], U16, name="offsets%d" % d)
             nc.sync.dma_start(offsets[:], pos)
             lists.append(offsets)
-        a_raw += [load_rows("a%d" % (2 + d), aT[:, d * T + PIECE : (d + 1) * T]) for d in range(2)]
+        w3_raw = load_rows("w3", w3)
+        a_raw = [load_rows("a%d" % u, aT[:, c0 : c0 + PIECE]) for u, c0 in enumerate((0, T, PIECE, T + PIECE))]
         w2_raw = sb.tile([P, PACK, N], F32, name="w2_raw")
         w2_rows = w2.rearrange("(q t r) n -> r q t n", t=PACK, r=4)
         for r in range(4):
             nc.sync.dma_start(out=w2_raw[r:P:4], in_=w2_rows[r])
 
-        w3_bf = sb.tile([P, PACK * PASS], BF16, name="w3_bf", align_bytes=64)
-        w3_dst = w3_bf[:].rearrange("p (t q r j) -> p t q j r", t=PACK, r=4, j=PACK)
-        w3_src = w3_raw[:].rearrange("p j (q t r) -> p t q j r", t=PACK, r=4)
-        cast("v", w3_dst[:, 0:2], w3_src[:, 0:2])
-        cast("s", w3_dst[:, 2:4], w3_src[:, 2:4])
-        w3_codes, w3_scales = quantise("w3", w3_bf[:], H)
+        h_banks = [ps.tile([P, T], F32, name="h_bank%d" % t, tag="b%d" % t) for t in range(PACK)]
+        w1_q = [weight_planes("w1_%d" % g, w1_raw[g], "vsvs") for g in range(2)]
+        for g in range(2):
+            for t in range(PACK):
+                wc, wsc = w1_q[g][t]
+                nc.tensor.matmul_mx(out=h_banks[t][:], lhsT=wc[:].bitcast(FP8X4), lhsT_scale=wsc[:],
+                                    rhs=xw[g][:].bitcast(FP8X4), rhs_scale=xs[:, g * T : (g + 1) * T],
+                                    start=(g == 0), stop=(g == 1))
+        h = []
+
+        def activate(t, tag):
+            ht = sb.tile([P, T], F32, name="h%d" % t, tag=tag)
+            nc.scalar.activation(ht[:], h_banks[t][:], SILU)
+            h.append(ht)
 
         def filters(u, engine, tags):
             g = plain_cast("a%d" % u, a_raw[u], PIECE, engine, "a%d_bf" % u)
@@ -123,22 +129,6 @@ def tile_picked_wdime_silu_l_kernel(tc, x_words, x_scales, aT, w1, w3, w2, pos1,
             f_sb = sb.tile([P, 2 * PIECE], F32, name=name, tag=tag or name)
             nc.scalar.copy(out=f_sb[:], in_=bank[:])
             return f_sb
-
-        f0 = filters(0, "v", ("b4", "b5"))
-        f0_sb = [to_sbuf("f0_sb%d" % i, f0[i]) for i in range(2)]
-        h_banks = [ps.tile([P, T], F32, name="h_bank%d" % t, tag="b%d" % t) for t in range(PACK)]
-        w1_q = [weight_planes("w1_%d" % g, w1_raw[g], "vsvs") for g in range(2)]
-        for g in range(2):
-            for t in range(PACK):
-                wc, wsc = w1_q[g][t]
-                nc.tensor.matmul_mx(out=h_banks[t][:], lhsT=wc[:].bitcast(FP8X4), lhsT_scale=wsc[:],
-                                    rhs=xw[g][:].bitcast(FP8X4), rhs_scale=xs[:, g * T : (g + 1) * T],
-                                    start=(g == 0), stop=(g == 1))
-        h = []
-        for t in range(PACK):
-            ht = sb.tile([P, T], F32, name="h%d" % t)
-            nc.scalar.activation(ht[:], h_banks[t][:], SILU)
-            h.append(ht)
 
         def looked_up(t, d, v0, width):
             return h[t][:].indirect(lists[d][:, v0 // 16 : (v0 + width) // 16])
@@ -185,25 +175,42 @@ def tile_picked_wdime_silu_l_kernel(tc, x_words, x_scales, aT, w1, w3, w2, pos1,
             nc.scalar.activation(o[:], bank[:], SILU)
             nc.sync.dma_start(out=out.rearrange("(m p) v -> p m v", p=P)[:, :, v0 : v0 + width], in_=o[:])
 
-        f1 = filters(1, "v", ("b6", "b7"))
+        activate(0, "h0")
+        activate(1, "h1")
+        activate(2, "h2")
+        w3_bf = sb.tile([P, PACK * PASS], BF16, name="w3_bf", align_bytes=64)
+        w3_dst = w3_bf[:].rearrange("p (t q r j) -> p t q j r", t=PACK, r=4, j=PACK)
+        w3_src = w3_raw[:].rearrange("p j (q t r) -> p t q j r", t=PACK, r=4)
+        cast("v", w3_dst[:, 0:1], w3_src[:, 0:1])
+        cast("s", w3_dst[:, 1:4], w3_src[:, 1:4])
+        w3_codes, w3_scales = quantise("w3", w3_bf[:], H)
+
+        f0 = filters(0, "s", ("b4", "b5"))
+        activate(3, "w3_raw")
+        f1 = filters(1, "s", ("b6", "b7"))
         f2 = filters(2, "s", ("b0", "b1"))
-        f1_sb = [to_sbuf("f1_sb%d" % i, f1[i], (None, "a2_raw")[i]) for i in range(2)]
         f3 = filters(3, "s", ("b2", "b3"))
         f2_sb = [to_sbuf("f2_sb%d" % i, f2[i]) for i in range(2)]
         w2_bf = plain_cast("w2", w2_raw, N, "s", "w2_bf")
         w2_codes, w2_scales = quantise("w2", w2_bf[:], N)
         f3_sb = [to_sbuf("f3_sb0", f3[0])]
 
-        def fused(name, f_sb, d, v0, tag):
-            prod = sb.tile([P, PACK, PIECE], F32, name=name, tag=tag, align_bytes=64)
+        g = [[sb.tile([P, 2 * PIECE], F32, name="g%d_%d" % (d, i)) for i in range(2)] for d in range(2)]
+        for t in range(PACK):
+            for d in range(2):
+                nc.vector.tensor_copy(g[d][t // 2][:, (t % 2) * PIECE : (t % 2 + 1) * PIECE], looked_up(t, d, 0, PIECE))
+        pa = [[times_bank("pa0_%d" % i, g[0][i], f0[i]) for i in range(2)], [times_bank("pa1_0", g[1][0], f1[0])]]
+        pa[1].append(times_bank("pa1_1", g[1][1], f1[1]))
+
+        def fused(name, f_sb, d, v0):
+            prod = sb.tile([P, PACK, PIECE], F32, name=name)
             for t in range(PACK):
                 nc.vector.tensor_tensor(prod[:, t, :], looked_up(t, d, v0, PIECE), f_sb[t // 2][:, (t % 2) * PIECE : (t % 2 + 1) * PIECE], MULT)
             return prod
 
-        pa = [fused("pa0", f0_sb, 0, 0, "pa0"), fused("pa1", f1_sb, 1, 0, "pa1")]
-        za = add_on_tensor("za", lambda t, d, b: pa[d][:, t, b * P : (b + 1) * P], 2, ("b4", "b5"), "b6", lambda: f3_sb.append(to_sbuf("f3_sb1", f3[1], "za_t1")))
+        za = add_on_tensor("za", lambda t, d, b: pa[d][t // 2][:, (t % 2) * PIECE + b * P : (t % 2) * PIECE + (b + 1) * P], 2, ("b4", "b5"), "b6", lambda: f3_sb.append(to_sbuf("f3_sb1", f3[1], "za_t1")))
         project("oa", quantise("za", za[:], PIECE), 0, PIECE, "b7")
-        pb = [fused("pb0", f2_sb, 0, PIECE, "pb0"), fused("pb1", f3_sb, 1, PIECE, "pb1")]
-        zb = [add_on_vector("zb%d" % s, pb[0][:, :, s * P : (s + 1) * P], pb[1][:, :, s * P : (s + 1) * P], P, ("zb0", "zb1")[s]) for s in range(2)]
+        pb = [fused("pb0", f2_sb, 0, PIECE), fused("pb1", f3_sb, 1, PIECE)]
+        zb = [add_on_vector("zb%d" % s, pb[0][:, :, s * P : (s + 1) * P], pb[1][:, :, s * P : (s + 1) * P], P, "zb%d" % s) for s in range(2)]
         for s in range(2):
             project("ob%d" % s, quantise("zb%d" % s, zb[s][:], P), PIECE + s * P, P, "b%d" % s)

@@ -20,7 +20,10 @@ ADD = mybir.AluOpType.add
 P = 128
 PACK = 4
 PASS = P * PACK
-PIECE = 256
+RUN = 4
+HALF = T // 2
+PER_COLUMN = 16
+W3_PLANES_ON_VECTOR = 1
 
 
 def tile_picked_wdime_silu_l_kernel(tc, x_words, x_scales, aT, w1, w3, w2, pos1, pos2, out):
@@ -29,12 +32,6 @@ def tile_picked_wdime_silu_l_kernel(tc, x_words, x_scales, aT, w1, w3, w2, pos1,
         sb = ctx.enter_context(tc.tile_pool(name="sb", bufs=1))
         ps = ctx.enter_context(tc.psum_pool(name="ps", bufs=1))
 
-        def cast(engine, dst, src):
-            if engine == "v":
-                nc.vector.tensor_copy(out=dst, in_=src)
-            else:
-                nc.scalar.copy(out=dst, in_=src)
-
         def quantise(name, grouped, width):
             codes = sb.tile([P, width], U32, name=name + "_codes", align_bytes=64)
             scales = sb.tile([P, width], U8, name=name + "_scales", align_bytes=64)
@@ -42,175 +39,210 @@ def tile_picked_wdime_silu_l_kernel(tc, x_words, x_scales, aT, w1, w3, w2, pos1,
             return codes, scales
 
         def load_rows(name, rows):
-            width = rows.shape[1]
-            raw = sb.tile([P, PACK, width], F32, name=name + "_raw")
+            raw = sb.tile([P, PACK, rows.shape[1]], F32, name=name + "_raw")
             nc.sync.dma_start(out=raw[:], in_=rows.rearrange("(p j) c -> p j c", j=PACK))
             return raw
-
-        def weight_planes(name, raw, engines):
-            src = raw[:].rearrange("p j (q t r) -> p t q j r", t=PACK, r=4)
-            planes = []
-            for t in range(PACK):
-                g = sb.tile([P, P * PACK], BF16, name="%s_bf%d" % (name, t), align_bytes=64)
-                cast(engines[t], g[:].rearrange("p (q r j) -> p q j r", r=4, j=PACK), src[:, t])
-                planes.append(quantise("%s_%d" % (name, t), g[:], P))
-            return planes
-
-        def plain_cast(name, raw, width, engine, tag):
-            g = sb.tile([P, width * PACK], BF16, name=name + "_bf", tag=tag, align_bytes=64)
-            cast(engine, g[:].rearrange("p (c r j) -> p c j r", r=4, j=PACK), raw[:].rearrange("p j (c r) -> p c j r", r=4))
-            return g
-
-        warm = sb.tile([P, 1], F32, name="warm")
-        nc.vector.memset(warm[:], 0.0)
-        warm2 = sb.tile([P, 1], F32, name="warm2")
-        nc.scalar.activation(warm2[:], warm[:], SILU)
-
-        xs = sb.tile([P, 2 * T], U8, name="xs", align_bytes=64)
-        nc.gpsimd.memset(xs[:].bitcast(I32), 0)
-        ident = sb.tile([P, P], F32, name="ident")
-        make_identity(nc, ident[:])
 
         def load_words(g):
             words = sb.tile([P, T], U32, name="xw%d" % g, align_bytes=64)
             nc.sync.dma_start(out=words[:].bitcast(I32), in_=x_words[g].rearrange("p c r -> p (c r)").bitcast(I32))
             return words
 
+        def round_and_quantise(name, raw, width):
+            grouped = sb.tile([P, width * PACK], BF16, name=name + "_bf", align_bytes=64)
+            nc.scalar.copy(
+                out=grouped[:].rearrange("p (c r j) -> p c j r", r=RUN, j=PACK),
+                in_=raw[:].rearrange("p j (c r) -> p c j r", r=RUN),
+            )
+            return quantise(name, grouped[:], width)
+
+        warm_in = sb.tile([P, 1], F32, name="warm")
+        nc.vector.memset(warm_in[:], 0.0)
+        warm_out = sb.tile([P, 1], F32, name="warm2")
+        nc.scalar.activation(warm_out[:], warm_in[:], SILU)
+
+        x_planes = sb.tile([P, T], U8, name="xs", align_bytes=64)
+        nc.gpsimd.memset(x_planes[:].bitcast(I32), 0)
+        ident = sb.tile([P, P], F32, name="ident")
+        make_identity(nc, ident[:])
+
         w1_raw = [load_rows("w1_0", w1[0:PASS, :])]
         for q in range(4):
             nc.sync.dma_start(
-                out=xs[32 * q : 32 * q + 4, :].bitcast(I32).rearrange("r (z c) -> r z c", z=2),
-                in_=x_scales[:, 4 * q : 4 * q + 4, :].bitcast(I32).rearrange("z r c -> r z c"),
+                out=x_planes[32 * q : 32 * q + 8, :].bitcast(I32),
+                in_=x_scales[:, 4 * q : 4 * q + 4, :].bitcast(I32),
             )
-        xw = [load_words(0)]
+        x_codes = [load_words(0)]
         w1_raw.append(load_rows("w1_1", w1[PASS : 2 * PASS, :]))
-        xw.append(load_words(1))
+        x_codes.append(load_words(1))
         lists = []
         for d, pos in enumerate((pos1, pos2)):
-            offsets = sb.tile([P, T // 16], U16, name="offsets%d" % d)
+            offsets = sb.tile([P, T // PER_COLUMN], U16, name="offsets%d" % d)
             nc.sync.dma_start(offsets[:], pos)
             lists.append(offsets)
         w3_raw = load_rows("w3", w3)
-        a_raw = [load_rows("a%d" % u, aT[:, c0 : c0 + PIECE]) for u, c0 in enumerate((0, T, PIECE, T + PIECE))]
+        a_raw = [
+            load_rows("a%d" % (2 * half + d), aT[:, d * T + half * HALF : d * T + (half + 1) * HALF])
+            for half in range(2)
+            for d in range(2)
+        ]
         w2_raw = sb.tile([P, PACK, N], F32, name="w2_raw")
         w2_rows = w2.rearrange("(q t r) n -> r q t n", t=PACK, r=4)
         for r in range(4):
             nc.sync.dma_start(out=w2_raw[r:P:4], in_=w2_rows[r])
 
         h_banks = [ps.tile([P, T], F32, name="h_bank%d" % t, tag="b%d" % t) for t in range(PACK)]
-        w1_q = [weight_planes("w1_%d" % g, w1_raw[g], "vsvs") for g in range(2)]
+        w1_q = []
+        for g in range(2):
+            src = w1_raw[g][:].rearrange("p j (q t r) -> p t q j r", t=PACK, r=RUN)
+            for t in range(PACK):
+                grouped = sb.tile([P, PASS], BF16, name="w1_%d_bf%d" % (g, t), align_bytes=64)
+                rounds = nc.scalar.copy if t % 2 else nc.vector.tensor_copy
+                rounds(out=grouped[:].rearrange("p (q r j) -> p q j r", r=RUN, j=PACK), in_=src[:, t])
+                w1_q.append(quantise("w1_%d_%d" % (g, t), grouped[:], P))
         for g in range(2):
             for t in range(PACK):
-                wc, wsc = w1_q[g][t]
-                nc.tensor.matmul_mx(out=h_banks[t][:], lhsT=wc[:].bitcast(FP8X4), lhsT_scale=wsc[:],
-                                    rhs=xw[g][:].bitcast(FP8X4), rhs_scale=xs[:, g * T : (g + 1) * T],
-                                    start=(g == 0), stop=(g == 1))
-        h = []
+                codes, scales = w1_q[PACK * g + t]
+                nc.tensor.matmul_mx(
+                    out=h_banks[t][:],
+                    lhsT=codes[:].bitcast(FP8X4),
+                    lhsT_scale=scales[:],
+                    rhs=x_codes[g][:].bitcast(FP8X4),
+                    rhs_scale=x_planes[4 * g : P, :],
+                    start=(g == 0),
+                    stop=(g == 1),
+                )
 
         def activate(t, tag):
-            ht = sb.tile([P, T], F32, name="h%d" % t, tag=tag)
-            nc.scalar.activation(ht[:], h_banks[t][:], SILU)
-            h.append(ht)
+            plane = sb.tile([P, T], F32, name="h%d" % t, tag=tag)
+            nc.scalar.activation(plane[:], h_banks[t][:], SILU)
+            return plane
 
-        def filters(u, engine, tags):
-            g = plain_cast("a%d" % u, a_raw[u], PIECE, engine, "a%d_bf" % u)
-            codes, scales = quantise("a%d" % u, g[:], PIECE)
+        h = [activate(t, "h%d" % t) for t in range(PACK - 1)]
+
+        w3_bf = sb.tile([P, PACK * PASS], BF16, name="w3_bf", align_bytes=64)
+        w3_dst = w3_bf[:].rearrange("p (t q r j) -> p t q j r", t=PACK, r=RUN, j=PACK)
+        w3_src = w3_raw[:].rearrange("p j (q t r) -> p t q j r", t=PACK, r=RUN)
+        nc.vector.tensor_copy(out=w3_dst[:, 0:W3_PLANES_ON_VECTOR], in_=w3_src[:, 0:W3_PLANES_ON_VECTOR])
+        nc.scalar.copy(out=w3_dst[:, W3_PLANES_ON_VECTOR:PACK], in_=w3_src[:, W3_PLANES_ON_VECTOR:PACK])
+        w3_codes, w3_scales = quantise("w3", w3_bf[:], H)
+
+        def filters(piece, tags):
+            codes, scales = round_and_quantise("a%d" % piece, a_raw[piece], HALF)
             banks = []
-            for half in range(2):
-                bank = ps.tile([P, 2 * PIECE], F32, name="f_bank", tag=tags[half])
+            for b in range(2):
+                bank = ps.tile([P, 2 * HALF], F32, name="f_bank", tag=tags[b])
                 for s in range(2):
-                    cols = slice((2 * half + s) * P, (2 * half + s + 1) * P)
-                    nc.tensor.matmul_mx(out=bank[:, s * PIECE : (s + 1) * PIECE], lhsT=w3_codes[:, cols].bitcast(FP8X4), lhsT_scale=w3_scales[:, cols],
-                                        rhs=codes[:].bitcast(FP8X4), rhs_scale=scales[:], start=True, stop=True)
+                    cols = slice((2 * b + s) * P, (2 * b + s + 1) * P)
+                    nc.tensor.matmul_mx(
+                        out=bank[:, s * HALF : (s + 1) * HALF],
+                        lhsT=w3_codes[:, cols].bitcast(FP8X4),
+                        lhsT_scale=w3_scales[:, cols],
+                        rhs=codes[:].bitcast(FP8X4),
+                        rhs_scale=scales[:],
+                        start=True,
+                        stop=True,
+                    )
                 banks.append(bank)
             return banks
 
-        def to_sbuf(name, bank, tag=None):
-            f_sb = sb.tile([P, 2 * PIECE], F32, name=name, tag=tag or name)
-            nc.scalar.copy(out=f_sb[:], in_=bank[:])
-            return f_sb
+        def to_sbuf(piece):
+            copies = []
+            for b in range(2):
+                staged = sb.tile([P, 2 * HALF], F32, name="f%d_sb%d" % (piece, b))
+                nc.scalar.copy(out=staged[:], in_=f_banks[piece][b][:])
+                copies.append(staged)
+            return copies
 
-        def looked_up(t, d, v0, width):
-            return h[t][:].indirect(lists[d][:, v0 // 16 : (v0 + width) // 16])
+        f_banks = [filters(0, ("b4", "b5"))]
+        h.append(activate(PACK - 1, "w3_raw"))
+        f_banks.append(filters(1, ("b6", "b7")))
+        f_banks.append(filters(2, ("b0", "b1")))
+        f_banks.append(filters(3, ("b2", "b3")))
+        f_sb = [to_sbuf(2)]
+        w2_codes, w2_scales = round_and_quantise("w2", w2_raw, N)
+        f_sb.append(to_sbuf(3))
 
-        def times_bank(name, g, bank):
-            prod = sb.tile([P, 2 * PIECE], F32, name=name)
-            nc.vector.tensor_tensor(prod[:], g[:], bank[:], MULT)
-            return prod
+        def looked_up(t, d, half):
+            columns = HALF // PER_COLUMN
+            return h[t][:].indirect(lists[d][:, half * columns : (half + 1) * columns])
 
-        def add_on_vector(name, pa, pb, width, tag):
-            z = sb.tile([P, width * PACK], BF16, name=name, tag=tag, align_bytes=64)
-            nc.vector.tensor_tensor(z[:].rearrange("p (c r t) -> p c t r", r=4, t=PACK),
-                                    pa.rearrange("p t (c r) -> p c t r", r=4), pb.rearrange("p t (c r) -> p c t r", r=4), ADD)
-            return z
+        def in_pair(t):
+            return slice((t % 2) * HALF, (t % 2 + 1) * HALF)
 
-        def add_on_tensor(name, terms, blocks, tags, back_tag, between):
-            back = ps.tile([P, blocks, 2, P], F32, name=name + "_back", tag=back_tag)
-            turned = []
-            for b in range(blocks):
-                bank = ps.tile([P, PACK, P], F32, name=name + "_sum", tag=tags[b])
-                for t in range(PACK):
-                    for d in range(2):
-                        nc.tensor.matmul(bank[:, t, :], lhsT=terms(t, d, b), rhs=ident[:], is_transpose=True, start=(d == 0), stop=(d == 1))
-                zt = sb.tile([P, PACK * P], BF16, name="%s_t%d" % (name, b))
-                nc.scalar.copy(out=zt[:].rearrange("v (u p e) -> v u p e", u=2, e=2), in_=bank[:].rearrange("v (u e) p -> v u p e", u=2))
-                turned.append(zt)
-            for b in range(blocks):
-                words = turned[b][:].bitcast(F32)
-                for u in range(2):
-                    nc.tensor.transpose(back[:, b, u, :], words[:, u * P : (u + 1) * P], ident[:])
-            between()
-            z = sb.tile([P, blocks * P * PACK], BF16, name=name, align_bytes=64)
-            nc.scalar.copy(out=z[:].bitcast(F32).rearrange("p (b v u) -> p b v u", b=blocks, u=2), in_=back[:].rearrange("p b u v -> p b v u"))
-            return z
-
-        def project(name, z_q, v0, width, tag):
-            codes, scales = z_q
+        def project(name, codes, scales, v0, width, tag):
             bank = ps.tile([P, 2, width], F32, name=name + "_bank", tag=tag)
-            for m in range(2):
-                nc.tensor.matmul_mx(out=bank[:, m, :], lhsT=w2_codes[:, m * P : (m + 1) * P].bitcast(FP8X4),
-                                    lhsT_scale=w2_scales[:, m * P : (m + 1) * P],
-                                    rhs=codes[:].bitcast(FP8X4), rhs_scale=scales[:], start=True, stop=True)
-            o = sb.tile([P, 2, width], F32, name=name + "_o")
-            nc.scalar.activation(o[:], bank[:], SILU)
-            nc.sync.dma_start(out=out.rearrange("(m p) v -> p m v", p=P)[:, :, v0 : v0 + width], in_=o[:])
+            for m in range(N // P):
+                nc.tensor.matmul_mx(
+                    out=bank[:, m, :],
+                    lhsT=w2_codes[:, m * P : (m + 1) * P].bitcast(FP8X4),
+                    lhsT_scale=w2_scales[:, m * P : (m + 1) * P],
+                    rhs=codes[:].bitcast(FP8X4),
+                    rhs_scale=scales[:],
+                    start=True,
+                    stop=True,
+                )
+            result = sb.tile([P, 2, width], F32, name=name + "_o")
+            nc.scalar.activation(result[:], bank[:], SILU)
+            nc.sync.dma_start(out=out.rearrange("(m p) v -> p m v", p=P)[:, :, v0 : v0 + width], in_=result[:])
 
-        activate(0, "h0")
-        activate(1, "h1")
-        activate(2, "h2")
-        w3_bf = sb.tile([P, PACK * PASS], BF16, name="w3_bf", align_bytes=64)
-        w3_dst = w3_bf[:].rearrange("p (t q r j) -> p t q j r", t=PACK, r=4, j=PACK)
-        w3_src = w3_raw[:].rearrange("p j (q t r) -> p t q j r", t=PACK, r=4)
-        cast("v", w3_dst[:, 0:1], w3_src[:, 0:1])
-        cast("s", w3_dst[:, 1:4], w3_src[:, 1:4])
-        w3_codes, w3_scales = quantise("w3", w3_bf[:], H)
-
-        f0 = filters(0, "s", ("b4", "b5"))
-        activate(3, "w3_raw")
-        f1 = filters(1, "s", ("b6", "b7"))
-        f2 = filters(2, "s", ("b0", "b1"))
-        f3 = filters(3, "s", ("b2", "b3"))
-        f2_sb = [to_sbuf("f2_sb%d" % i, f2[i]) for i in range(2)]
-        w2_bf = plain_cast("w2", w2_raw, N, "s", "w2_bf")
-        w2_codes, w2_scales = quantise("w2", w2_bf[:], N)
-        f3_sb = [to_sbuf("f3_sb0", f3[0])]
-
-        g = [[sb.tile([P, 2 * PIECE], F32, name="g%d_%d" % (d, i)) for i in range(2)] for d in range(2)]
+        picked = [[sb.tile([P, 2 * HALF], F32, name="g%d_%d" % (d, b)) for b in range(2)] for d in range(2)]
         for t in range(PACK):
             for d in range(2):
-                nc.vector.tensor_copy(g[d][t // 2][:, (t % 2) * PIECE : (t % 2 + 1) * PIECE], looked_up(t, d, 0, PIECE))
-        pa = [[times_bank("pa0_%d" % i, g[0][i], f0[i]) for i in range(2)], [times_bank("pa1_0", g[1][0], f1[0])]]
-        pa[1].append(times_bank("pa1_1", g[1][1], f1[1]))
+                nc.vector.tensor_copy(picked[d][t // 2][:, in_pair(t)], looked_up(t, d, 0))
+        terms = [[], []]
+        for d in range(2):
+            for b in range(2):
+                product = sb.tile([P, 2 * HALF], F32, name="pa%d_%d" % (d, b))
+                nc.vector.tensor_tensor(product[:], picked[d][b][:], f_banks[d][b][:], MULT)
+                terms[d].append(product)
 
-        def fused(name, f_sb, d, v0):
-            prod = sb.tile([P, PACK, PIECE], F32, name=name)
+        blocks = HALF // P
+        back = ps.tile([P, blocks, 2, P], F32, name="za_back", tag="b6")
+        turned = []
+        for blk in range(blocks):
+            bank = ps.tile([P, PACK, P], F32, name="za_sum", tag=("b4", "b5")[blk])
             for t in range(PACK):
-                nc.vector.tensor_tensor(prod[:, t, :], looked_up(t, d, v0, PIECE), f_sb[t // 2][:, (t % 2) * PIECE : (t % 2 + 1) * PIECE], MULT)
-            return prod
+                for d in range(2):
+                    term = terms[d][t // 2][:, in_pair(t)][:, blk * P : (blk + 1) * P]
+                    nc.tensor.matmul(bank[:, t, :], lhsT=term, rhs=ident[:], is_transpose=True, start=(d == 0), stop=(d == 1))
+            pairs = sb.tile([P, PACK * P], BF16, name="za_t%d" % blk)
+            nc.scalar.copy(
+                out=pairs[:].rearrange("v (u p e) -> v u p e", u=2, e=2),
+                in_=bank[:].rearrange("v (u e) p -> v u p e", u=2),
+            )
+            turned.append(pairs)
+        for blk in range(blocks):
+            words = turned[blk][:].bitcast(F32)
+            for u in range(2):
+                nc.tensor.transpose(back[:, blk, u, :], words[:, u * P : (u + 1) * P], ident[:])
+        z = sb.tile([P, HALF * PACK], BF16, name="za", align_bytes=64)
+        nc.scalar.copy(
+            out=z[:].bitcast(F32).rearrange("p (b v u) -> p b v u", b=blocks, u=2),
+            in_=back[:].rearrange("p b u v -> p b v u"),
+        )
+        z_blocks = [z[:, blk * PASS : (blk + 1) * PASS] for blk in range(blocks)]
+        first_codes = sb.tile([P, HALF], U32, name="za_codes", align_bytes=64)
+        first_scales = sb.tile([P, HALF], U8, name="za_scales", align_bytes=64)
+        for blk in range(blocks):
+            cols = slice(blk * P, (blk + 1) * P)
+            nc.vector.quantize_mx(out=first_codes[:, cols].bitcast(FP8X4), scales=first_scales[:, cols], in_=z_blocks[blk])
+        project("oa", first_codes, first_scales, 0, HALF, "b7")
 
-        za = add_on_tensor("za", lambda t, d, b: pa[d][t // 2][:, (t % 2) * PIECE + b * P : (t % 2) * PIECE + (b + 1) * P], 2, ("b4", "b5"), "b6", lambda: f3_sb.append(to_sbuf("f3_sb1", f3[1], "za_t1")))
-        project("oa", quantise("za", za[:], PIECE), 0, PIECE, "b7")
-        pb = [fused("pb0", f2_sb, 0, PIECE), fused("pb1", f3_sb, 1, PIECE)]
-        zb = [add_on_vector("zb%d" % s, pb[0][:, :, s * P : (s + 1) * P], pb[1][:, :, s * P : (s + 1) * P], P, "zb%d" % s) for s in range(2)]
-        for s in range(2):
-            project("ob%d" % s, quantise("zb%d" % s, zb[s][:], P), PIECE + s * P, P, "b%d" % s)
+        fused = []
+        for d in range(2):
+            product = sb.tile([P, PACK, HALF], F32, name="pb%d" % d)
+            for t in range(PACK):
+                nc.vector.tensor_tensor(product[:, t, :], looked_up(t, d, 1), f_sb[d][t // 2][:, in_pair(t)], MULT)
+            fused.append(product)
+        for blk in range(blocks):
+            cols = slice(blk * P, (blk + 1) * P)
+            nc.vector.tensor_tensor(
+                z_blocks[blk].rearrange("p (c r t) -> p c t r", r=RUN, t=PACK),
+                fused[0][:, :, cols].rearrange("p t (c r) -> p c t r", r=RUN),
+                fused[1][:, :, cols].rearrange("p t (c r) -> p c t r", r=RUN),
+                ADD,
+            )
+        for blk in range(blocks):
+            codes, scales = quantise("zb%d" % blk, z_blocks[blk], P)
+            project("ob%d" % blk, codes, scales, HALF + blk * P, P, "b%d" % blk)

@@ -1,7 +1,6 @@
 from contextlib import ExitStack
 
 import concourse.mybir as mybir
-from concourse.masks import make_identity
 
 K, T, H, N, J, U = 1024, 512, 512, 256, 512, 1024
 FLOPS = 2 * (K * H * T + J * H * U + H * N * T)
@@ -13,6 +12,7 @@ U32 = mybir.dt.uint32
 U16 = mybir.dt.uint16
 U8 = mybir.dt.uint8
 FP8X4 = mybir.dt.float8_e4m3fn_x4
+COPY = mybir.ActivationFunctionType.Copy
 SILU = mybir.ActivationFunctionType.Silu
 MULT = mybir.AluOpType.mult
 ADD = mybir.AluOpType.add
@@ -23,7 +23,6 @@ PASS = P * PACK
 RUN = 4
 HALF = T // 2
 PER_COLUMN = 16
-W3_PLANES_ON_VECTOR = 1
 
 
 def tile_picked_wdime_silu_l_kernel(tc, x_words, x_scales, aT, w1, w3, w2, pos1, pos2, out):
@@ -50,7 +49,7 @@ def tile_picked_wdime_silu_l_kernel(tc, x_words, x_scales, aT, w1, w3, w2, pos1,
 
         def round_and_quantise(name, raw, width):
             grouped = sb.tile([P, width * PACK], BF16, name=name + "_bf", align_bytes=64)
-            nc.scalar.copy(
+            nc.vector.tensor_copy(
                 out=grouped[:].rearrange("p (c r j) -> p c j r", r=RUN, j=PACK),
                 in_=raw[:].rearrange("p j (c r) -> p c j r", r=RUN),
             )
@@ -63,8 +62,6 @@ def tile_picked_wdime_silu_l_kernel(tc, x_words, x_scales, aT, w1, w3, w2, pos1,
 
         x_planes = sb.tile([P, T], U8, name="xs", align_bytes=64)
         nc.gpsimd.memset(x_planes[:].bitcast(I32), 0)
-        ident = sb.tile([P, P], F32, name="ident")
-        make_identity(nc, ident[:])
 
         w1_raw = [load_rows("w1_0", w1[0:PASS, :])]
         for q in range(4):
@@ -113,18 +110,17 @@ def tile_picked_wdime_silu_l_kernel(tc, x_words, x_scales, aT, w1, w3, w2, pos1,
                     stop=(g == 1),
                 )
 
-        def activate(t, tag):
-            plane = sb.tile([P, T], F32, name="h%d" % t, tag=tag)
+        h = []
+        for t in range(PACK):
+            plane = sb.tile([P, T], F32, name="h%d" % t)
             nc.scalar.activation(plane[:], h_banks[t][:], SILU)
-            return plane
-
-        h = [activate(t, "h%d" % t) for t in range(PACK - 1)]
+            h.append(plane)
 
         w3_bf = sb.tile([P, PACK * PASS], BF16, name="w3_bf", align_bytes=64)
-        w3_dst = w3_bf[:].rearrange("p (t q r j) -> p t q j r", t=PACK, r=RUN, j=PACK)
-        w3_src = w3_raw[:].rearrange("p j (q t r) -> p t q j r", t=PACK, r=RUN)
-        nc.vector.tensor_copy(out=w3_dst[:, 0:W3_PLANES_ON_VECTOR], in_=w3_src[:, 0:W3_PLANES_ON_VECTOR])
-        nc.scalar.copy(out=w3_dst[:, W3_PLANES_ON_VECTOR:PACK], in_=w3_src[:, W3_PLANES_ON_VECTOR:PACK])
+        nc.vector.tensor_copy(
+            out=w3_bf[:].rearrange("p (t q r j) -> p t q j r", t=PACK, r=RUN, j=PACK),
+            in_=w3_raw[:].rearrange("p j (q t r) -> p t q j r", t=PACK, r=RUN),
+        )
         w3_codes, w3_scales = quantise("w3", w3_bf[:], H)
 
         def filters(piece, tags):
@@ -146,29 +142,17 @@ def tile_picked_wdime_silu_l_kernel(tc, x_words, x_scales, aT, w1, w3, w2, pos1,
                 banks.append(bank)
             return banks
 
-        def to_sbuf(piece):
-            copies = []
-            for b in range(2):
-                staged = sb.tile([P, 2 * HALF], F32, name="f%d_sb%d" % (piece, b))
-                nc.scalar.copy(out=staged[:], in_=f_banks[piece][b][:])
-                copies.append(staged)
-            return copies
-
-        f_banks = [filters(0, ("b4", "b5"))]
-        h.append(activate(PACK - 1, "w3_raw"))
-        f_banks.append(filters(1, ("b6", "b7")))
-        f_banks.append(filters(2, ("b0", "b1")))
-        f_banks.append(filters(3, ("b2", "b3")))
-        f_sb = [to_sbuf(2)]
+        f_banks = [
+            filters(0, ("b4", "b5")),
+            filters(1, ("b6", "b7")),
+            filters(2, ("b0", "b1")),
+            filters(3, ("b2", "b3")),
+        ]
         w2_codes, w2_scales = round_and_quantise("w2", w2_raw, N)
-        f_sb.append(to_sbuf(3))
 
         def looked_up(t, d, half):
             columns = HALF // PER_COLUMN
             return h[t][:].indirect(lists[d][:, half * columns : (half + 1) * columns])
-
-        def in_pair(t):
-            return slice((t % 2) * HALF, (t % 2 + 1) * HALF)
 
         def project(name, codes, scales, v0, width, tag):
             bank = ps.tile([P, 2, width], F32, name=name + "_bank", tag=tag)
@@ -186,63 +170,43 @@ def tile_picked_wdime_silu_l_kernel(tc, x_words, x_scales, aT, w1, w3, w2, pos1,
             nc.scalar.activation(result[:], bank[:], SILU)
             nc.sync.dma_start(out=out.rearrange("(m p) v -> p m v", p=P)[:, :, v0 : v0 + width], in_=result[:])
 
-        picked = [[sb.tile([P, 2 * HALF], F32, name="g%d_%d" % (d, b)) for b in range(2)] for d in range(2)]
-        for t in range(PACK):
+        picked = {}
+        for half in range(2):
             for d in range(2):
-                nc.vector.tensor_copy(picked[d][t // 2][:, in_pair(t)], looked_up(t, d, 0))
-        terms = [[], []]
-        for d in range(2):
-            for b in range(2):
-                product = sb.tile([P, 2 * HALF], F32, name="pa%d_%d" % (d, b))
-                nc.vector.tensor_tensor(product[:], picked[d][b][:], f_banks[d][b][:], MULT)
-                terms[d].append(product)
+                for b in range(2):
+                    pair = sb.tile([P, 2, HALF], F32, name="g%d_%d_%d" % (half, d, b))
+                    for s in range(2):
+                        nc.scalar.activation(pair[:, s, :], looked_up(2 * b + s, d, half), COPY)
+                    picked[half, d, b] = pair
 
-        blocks = HALF // P
-        back = ps.tile([P, blocks, 2, P], F32, name="za_back", tag="b6")
-        turned = []
-        for blk in range(blocks):
-            bank = ps.tile([P, PACK, P], F32, name="za_sum", tag=("b4", "b5")[blk])
-            for t in range(PACK):
-                for d in range(2):
-                    term = terms[d][t // 2][:, in_pair(t)][:, blk * P : (blk + 1) * P]
-                    nc.tensor.matmul(bank[:, t, :], lhsT=term, rhs=ident[:], is_transpose=True, start=(d == 0), stop=(d == 1))
-            pairs = sb.tile([P, PACK * P], BF16, name="za_t%d" % blk)
-            nc.scalar.copy(
-                out=pairs[:].rearrange("v (u p e) -> v u p e", u=2, e=2),
-                in_=bank[:].rearrange("v (u e) p -> v u p e", u=2),
-            )
-            turned.append(pairs)
-        for blk in range(blocks):
-            words = turned[blk][:].bitcast(F32)
-            for u in range(2):
-                nc.tensor.transpose(back[:, blk, u, :], words[:, u * P : (u + 1) * P], ident[:])
-        z = sb.tile([P, HALF * PACK], BF16, name="za", align_bytes=64)
-        nc.scalar.copy(
-            out=z[:].bitcast(F32).rearrange("p (b v u) -> p b v u", b=blocks, u=2),
-            in_=back[:].rearrange("p b u v -> p b v u"),
-        )
-        z_blocks = [z[:, blk * PASS : (blk + 1) * PASS] for blk in range(blocks)]
-        first_codes = sb.tile([P, HALF], U32, name="za_codes", align_bytes=64)
-        first_scales = sb.tile([P, HALF], U8, name="za_scales", align_bytes=64)
-        for blk in range(blocks):
-            cols = slice(blk * P, (blk + 1) * P)
-            nc.vector.quantize_mx(out=first_codes[:, cols].bitcast(FP8X4), scales=first_scales[:, cols], in_=z_blocks[blk])
-        project("oa", first_codes, first_scales, 0, HALF, "b7")
-
-        fused = []
-        for d in range(2):
-            product = sb.tile([P, PACK, HALF], F32, name="pb%d" % d)
-            for t in range(PACK):
-                nc.vector.tensor_tensor(product[:, t, :], looked_up(t, d, 1), f_sb[d][t // 2][:, in_pair(t)], MULT)
-            fused.append(product)
-        for blk in range(blocks):
-            cols = slice(blk * P, (blk + 1) * P)
+        def add_round(z, terms, cols):
             nc.vector.tensor_tensor(
-                z_blocks[blk].rearrange("p (c r t) -> p c t r", r=RUN, t=PACK),
-                fused[0][:, :, cols].rearrange("p t (c r) -> p c t r", r=RUN),
-                fused[1][:, :, cols].rearrange("p t (c r) -> p c t r", r=RUN),
+                z.rearrange("p (c r t) -> p c t r", r=RUN, t=PACK),
+                terms[0][:, :, cols].rearrange("p t (c r) -> p c t r", r=RUN),
+                terms[1][:, :, cols].rearrange("p t (c r) -> p c t r", r=RUN),
                 ADD,
             )
-        for blk in range(blocks):
-            codes, scales = quantise("zb%d" % blk, z_blocks[blk], P)
-            project("ob%d" % blk, codes, scales, HALF + blk * P, P, "b%d" % blk)
+
+        for half in range(2):
+            terms = []
+            for d in range(2):
+                product = sb.tile([P, PACK, HALF], F32, name="prod%d_%d" % (half, d))
+                for b in range(2):
+                    nc.vector.tensor_tensor(
+                        product[:, 2 * b : 2 * b + 2, :].rearrange("p t v -> p (t v)"),
+                        picked[half, d, b][:].rearrange("p t v -> p (t v)"),
+                        f_banks[2 * half + d][b][:],
+                        MULT,
+                    )
+                terms.append(product)
+            z = sb.tile([P, HALF * PACK], BF16, name="z%d" % half, align_bytes=64)
+            if half == 0:
+                add_round(z[:], terms, slice(0, HALF))
+                codes, scales = quantise("z0", z[:], HALF)
+                project("o0", codes, scales, 0, HALF, "b4")
+            else:
+                for blk in range(2):
+                    add_round(z[:, blk * PASS : (blk + 1) * PASS], terms, slice(blk * P, (blk + 1) * P))
+                for blk in range(2):
+                    codes, scales = quantise("z1_%d" % blk, z[:, blk * PASS : (blk + 1) * PASS], P)
+                    project("o1_%d" % blk, codes, scales, HALF + blk * P, P, "b%d" % (5 + blk))

@@ -31,14 +31,14 @@ def tile_picked_wdime_silu_l_kernel(tc, x_words, x_scales, aT, w1, w3, w2, pos1,
         sb = ctx.enter_context(tc.tile_pool(name="sb", bufs=1))
         ps = ctx.enter_context(tc.psum_pool(name="ps", bufs=1))
 
-        def quantise(name, grouped, width):
-            codes = sb.tile([P, width], U32, name=name + "_codes", align_bytes=64)
+        def quantise(name, grouped, width, tag=None):
+            codes = sb.tile([P, width], U32, name=name + "_codes", tag=tag or name + "_codes", align_bytes=64)
             scales = sb.tile([P, width], U8, name=name + "_scales", align_bytes=64)
             nc.vector.quantize_mx(out=codes[:].bitcast(FP8X4), scales=scales[:], in_=grouped)
             return codes, scales
 
         def load_rows(name, rows):
-            raw = sb.tile([P, PACK, rows.shape[1]], F32, name=name + "_raw")
+            raw = sb.tile([P, PACK, rows.shape[1]], F32, name=name + "_raw", align_bytes=64)
             nc.sync.dma_start(out=raw[:], in_=rows.rearrange("(p j) c -> p j c", j=PACK))
             return raw
 
@@ -47,13 +47,13 @@ def tile_picked_wdime_silu_l_kernel(tc, x_words, x_scales, aT, w1, w3, w2, pos1,
             nc.sync.dma_start(out=words[:].bitcast(I32), in_=x_words[g].rearrange("p c r -> p (c r)").bitcast(I32))
             return words
 
-        def round_and_quantise(name, raw, width):
-            grouped = sb.tile([P, width * PACK], BF16, name=name + "_bf", align_bytes=64)
-            nc.vector.tensor_copy(
+        def rounded(name, raw, width, copy, tag=None):
+            grouped = sb.tile([P, width * PACK], BF16, name=name + "_bf", tag=tag or name + "_bf", align_bytes=64)
+            copy(
                 out=grouped[:].rearrange("p (c r j) -> p c j r", r=RUN, j=PACK),
                 in_=raw[:].rearrange("p j (c r) -> p c j r", r=RUN),
             )
-            return quantise(name, grouped[:], width)
+            return grouped
 
         warm_in = sb.tile([P, 1], F32, name="warm")
         nc.vector.memset(warm_in[:], 0.0)
@@ -83,10 +83,10 @@ def tile_picked_wdime_silu_l_kernel(tc, x_words, x_scales, aT, w1, w3, w2, pos1,
             for half in range(2)
             for d in range(2)
         ]
-        w2_raw = sb.tile([P, PACK, N], F32, name="w2_raw")
-        w2_rows = w2.rearrange("(q t r) n -> r q t n", t=PACK, r=4)
-        for r in range(4):
-            nc.sync.dma_start(out=w2_raw[r:P:4], in_=w2_rows[r])
+        w2_raw = sb.tile([P, PACK, N], F32, name="w2_raw", align_bytes=64)
+        w2_rows = w2.rearrange("(q t r) n -> t q r n", t=PACK, r=4)
+        for t in range(PACK):
+            nc.sync.dma_start(out=w2_raw[:, t, :], in_=w2_rows[t])
 
         h_banks = [ps.tile([P, T], F32, name="h_bank%d" % t, tag="b%d" % t) for t in range(PACK)]
         w1_q = []
@@ -112,47 +112,41 @@ def tile_picked_wdime_silu_l_kernel(tc, x_words, x_scales, aT, w1, w3, w2, pos1,
 
         h = []
         for t in range(PACK):
-            plane = sb.tile([P, T], F32, name="h%d" % t)
+            plane = sb.tile([P, T], F32, name="h%d" % t, align_bytes=64)
             nc.scalar.activation(plane[:], h_banks[t][:], SILU)
             h.append(plane)
 
-        w3_bf = sb.tile([P, PACK * PASS], BF16, name="w3_bf", align_bytes=64)
-        nc.vector.tensor_copy(
-            out=w3_bf[:].rearrange("p (t q r j) -> p t q j r", t=PACK, r=RUN, j=PACK),
-            in_=w3_raw[:].rearrange("p j (q t r) -> p t q j r", t=PACK, r=RUN),
-        )
-        w3_codes, w3_scales = quantise("w3", w3_bf[:], H)
+        def gather(picked, t, d, v0, width, engine):
+            window = h[t][:].indirect(lists[d][:, v0 // PER_COLUMN : (v0 + width) // PER_COLUMN])
+            if engine is nc.vector:
+                nc.vector.tensor_copy(picked, window)
+            else:
+                nc.scalar.activation(picked, window, COPY)
 
-        def filters(piece, tags):
-            codes, scales = round_and_quantise("a%d" % piece, a_raw[piece], HALF)
-            banks = []
-            for b in range(2):
-                bank = ps.tile([P, 2 * HALF], F32, name="f_bank", tag=tags[b])
-                for s in range(2):
-                    cols = slice((2 * b + s) * P, (2 * b + s + 1) * P)
-                    nc.tensor.matmul_mx(
-                        out=bank[:, s * HALF : (s + 1) * HALF],
-                        lhsT=w3_codes[:, cols].bitcast(FP8X4),
-                        lhsT_scale=w3_scales[:, cols],
-                        rhs=codes[:].bitcast(FP8X4),
-                        rhs_scale=scales[:],
-                        start=True,
-                        stop=True,
-                    )
-                banks.append(bank)
-            return banks
+        def filters(codes, scales, c0, width, planes, tag):
+            bank = ps.tile([P, len(planes), width], F32, name="f_bank", tag=tag)
+            for s, t in enumerate(planes):
+                nc.tensor.matmul_mx(
+                    out=bank[:, s, :],
+                    lhsT=w3_codes[:, t * P : (t + 1) * P].bitcast(FP8X4),
+                    lhsT_scale=w3_scales[:, t * P : (t + 1) * P],
+                    rhs=codes[:, c0 : c0 + width].bitcast(FP8X4),
+                    rhs_scale=scales[:, c0 : c0 + width],
+                    start=True,
+                    stop=True,
+                )
+            return bank
 
-        f_banks = [
-            filters(0, ("b4", "b5")),
-            filters(1, ("b6", "b7")),
-            filters(2, ("b0", "b1")),
-            filters(3, ("b2", "b3")),
-        ]
-        w2_codes, w2_scales = round_and_quantise("w2", w2_raw, N)
+        def multiply(product, picked, bank):
+            nc.vector.tensor_tensor(product, picked, bank[:], MULT)
 
-        def looked_up(t, d, half):
-            columns = HALF // PER_COLUMN
-            return h[t][:].indirect(lists[d][:, half * columns : (half + 1) * columns])
+        def add_and_round(z, terms):
+            nc.vector.tensor_tensor(
+                z.rearrange("p (c r t) -> p c t r", r=RUN, t=PACK),
+                terms[0].rearrange("p t (c r) -> p c t r", r=RUN),
+                terms[1].rearrange("p t (c r) -> p c t r", r=RUN),
+                ADD,
+            )
 
         def project(name, codes, scales, v0, width, tag):
             bank = ps.tile([P, 2, width], F32, name=name + "_bank", tag=tag)
@@ -170,43 +164,52 @@ def tile_picked_wdime_silu_l_kernel(tc, x_words, x_scales, aT, w1, w3, w2, pos1,
             nc.scalar.activation(result[:], bank[:], SILU)
             nc.sync.dma_start(out=out.rearrange("(m p) v -> p m v", p=P)[:, :, v0 : v0 + width], in_=result[:])
 
-        picked = {}
-        for half in range(2):
-            for d in range(2):
-                for b in range(2):
-                    pair = sb.tile([P, 2, HALF], F32, name="g%d_%d_%d" % (half, d, b))
-                    for s in range(2):
-                        nc.scalar.activation(pair[:, s, :], looked_up(2 * b + s, d, half), COPY)
-                    picked[half, d, b] = pair
-
-        def add_round(z, terms, cols):
-            nc.vector.tensor_tensor(
-                z.rearrange("p (c r t) -> p c t r", r=RUN, t=PACK),
-                terms[0][:, :, cols].rearrange("p t (c r) -> p c t r", r=RUN),
-                terms[1][:, :, cols].rearrange("p t (c r) -> p c t r", r=RUN),
-                ADD,
-            )
-
-        for half in range(2):
-            terms = []
-            for d in range(2):
-                product = sb.tile([P, PACK, HALF], F32, name="prod%d_%d" % (half, d))
-                for b in range(2):
-                    nc.vector.tensor_tensor(
-                        product[:, 2 * b : 2 * b + 2, :].rearrange("p t v -> p (t v)"),
-                        picked[half, d, b][:].rearrange("p t v -> p (t v)"),
-                        f_banks[2 * half + d][b][:],
-                        MULT,
-                    )
-                terms.append(product)
-            z = sb.tile([P, HALF * PACK], BF16, name="z%d" % half, align_bytes=64)
-            if half == 0:
-                add_round(z[:], terms, slice(0, HALF))
-                codes, scales = quantise("z0", z[:], HALF)
-                project("o0", codes, scales, 0, HALF, "b4")
-            else:
-                for blk in range(2):
-                    add_round(z[:, blk * PASS : (blk + 1) * PASS], terms, slice(blk * P, (blk + 1) * P))
-                for blk in range(2):
-                    codes, scales = quantise("z1_%d" % blk, z[:, blk * PASS : (blk + 1) * PASS], P)
-                    project("o1_%d" % blk, codes, scales, HALF + blk * P, P, "b%d" % (5 + blk))
+        LOW, HIGH, ALL = (0, 1), (2, 3), (0, 1, 2, 3)
+        g = {(half, d): sb.tile([P, PACK, HALF], F32, name="g%d%d" % (half, d)) for half in range(2) for d in range(2)}
+        for half, d in ((0, 0), (0, 1), (1, 0)):
+            for t in range(PACK):
+                gather(g[half, d][:, t, :], t, d, half * HALF, HALF, nc.scalar)
+        for blk in range(2):
+            for t in range(PACK):
+                gather(g[1, 1][:, t, blk * P : (blk + 1) * P], t, 1, HALF + blk * P, P, nc.scalar)
+        w3_bf = sb.tile([P, PACK * PASS], BF16, name="w3_bf", align_bytes=64)
+        nc.vector.tensor_copy(
+            out=w3_bf[:].rearrange("p (t q r j) -> p t q j r", t=PACK, r=RUN, j=PACK),
+            in_=w3_raw[:].rearrange("p j (q t r) -> p t q j r", t=PACK, r=RUN),
+        )
+        w3_codes, w3_scales = quantise("w3", w3_bf[:], H)
+        a0 = quantise("a0", rounded("a0", a_raw[0], HALF, nc.vector.tensor_copy)[:], HALF)
+        f00 = [filters(*a0, 0, HALF, LOW, "b4"), filters(*a0, 0, HALF, HIGH, "b5")]
+        p00 = sb.tile([P, PACK, HALF], F32, name="p00")
+        p01 = sb.tile([P, PACK, HALF], F32, name="p01")
+        p10 = sb.tile([P, PACK, HALF], F32, name="p10")
+        staged = rounded("a1", a_raw[1], HALF, nc.vector.tensor_copy, "w3_bf")
+        multiply(p00[:, 0:2, :], g[0, 0][:, 0:2, :], f00[0])
+        a1 = quantise("a1", staged[:], HALF)
+        f01 = [filters(*a1, 0, HALF, LOW, "b6"), filters(*a1, 0, HALF, HIGH, "b7")]
+        multiply(p00[:, 2:4, :], g[0, 0][:, 2:4, :], f00[1])
+        staged = rounded("a2", a_raw[2], HALF, nc.vector.tensor_copy, "w3_bf")
+        multiply(p01[:, 0:2, :], g[0, 1][:, 0:2, :], f01[0])
+        a2 = quantise("a2", staged[:], HALF)
+        f10 = [filters(*a2, 0, HALF, LOW, "b0"), filters(*a2, 0, HALF, HIGH, "b1")]
+        multiply(p01[:, 2:4, :], g[0, 1][:, 2:4, :], f01[1])
+        staged = rounded("a3", a_raw[3], HALF, nc.vector.tensor_copy, "w3_bf")
+        z0 = sb.tile([P, HALF * PACK], BF16, name="z0", align_bytes=64)
+        add_and_round(z0[:], (p00[:], p01[:]))
+        a3 = quantise("a3", staged[:], HALF)
+        f11 = [filters(*a3, 0, P, ALL, "b2"), filters(*a3, P, P, ALL, "b3")]
+        z0_q = quantise("z0", z0[:], HALF)
+        staged = rounded("w2", w2_raw, N, nc.vector.tensor_copy, "w3_bf")
+        multiply(p10[:, 0:2, :], g[1, 0][:, 0:2, :], f10[0])
+        w2_codes, w2_scales = quantise("w2", staged[:], N)
+        project("o0", z0_q[0], z0_q[1], 0, HALF, "b4")
+        multiply(p10[:, 2:4, :], g[1, 0][:, 2:4, :], f10[1])
+        p11 = [sb.tile([P, PACK, P], F32, name="p11_%d" % blk) for blk in range(2)]
+        for blk in range(2):
+            multiply(p11[blk][:], g[1, 1][:, :, blk * P : (blk + 1) * P], f11[blk])
+        z1 = [sb.tile([P, PASS], BF16, name="z1_%d" % blk, align_bytes=64) for blk in range(2)]
+        for blk in range(2):
+            add_and_round(z1[blk][:], (p10[:, :, blk * P : (blk + 1) * P], p11[blk][:]))
+        for blk in range(2):
+            codes, scales = quantise("z1_%d" % blk, z1[blk][:], P)
+            project("o1_%d" % blk, codes, scales, HALF + blk * P, P, "b%d" % (5 + blk))

@@ -29,6 +29,7 @@ def tile_picked_wdime_silu_l_kernel(tc, x_words, x_scales, aT, w1, w3, w2, pos1,
     nc = tc.nc
     with ExitStack() as ctx:
         sb = ctx.enter_context(tc.tile_pool(name="sb", bufs=1))
+        shared = ctx.enter_context(tc.tile_pool(name="shared", bufs=1))
         ps = ctx.enter_context(tc.psum_pool(name="ps", bufs=1))
 
         def quantise(name, grouped, width, tag=None):
@@ -77,12 +78,10 @@ def tile_picked_wdime_silu_l_kernel(tc, x_words, x_scales, aT, w1, w3, w2, pos1,
             offsets = sb.tile([P, T // PER_COLUMN], U16, name="offsets%d" % d)
             nc.sync.dma_start(offsets[:], pos)
             lists.append(offsets)
+        pieces = [aT[:, d * T + half * HALF : d * T + (half + 1) * HALF] for half in range(2) for d in range(2)]
+        a_raw = [load_rows("a0", pieces[0])]
         w3_raw = load_rows("w3", w3)
-        a_raw = [
-            load_rows("a%d" % (2 * half + d), aT[:, d * T + half * HALF : d * T + (half + 1) * HALF])
-            for half in range(2)
-            for d in range(2)
-        ]
+        a_raw.extend(load_rows("a%d" % n, pieces[n]) for n in range(1, 4))
         w2_raw = sb.tile([P, PACK, N], F32, name="w2_raw", align_bytes=64)
         w2_rows = w2.rearrange("(q t r) n -> t q r n", t=PACK, r=4)
         for t in range(PACK):
@@ -140,8 +139,16 @@ def tile_picked_wdime_silu_l_kernel(tc, x_words, x_scales, aT, w1, w3, w2, pos1,
         def multiply(product, picked, bank):
             nc.vector.tensor_tensor(product, picked, bank[:], MULT)
 
-        def add_and_round(z, terms):
+        def multiply_woven(product, picked, bank):
             nc.vector.tensor_tensor(
+                product.rearrange("p (c r t) -> p c t r", r=4, t=PACK),
+                picked.rearrange("p t (c r) -> p c t r", r=4),
+                bank[:].rearrange("p t (c r) -> p c t r", r=4),
+                MULT,
+            )
+
+        def add_and_round(z, terms, engine):
+            engine.tensor_tensor(
                 z.rearrange("p (c r t) -> p c t r", r=RUN, t=PACK),
                 terms[0].rearrange("p t (c r) -> p c t r", r=RUN),
                 terms[1].rearrange("p t (c r) -> p c t r", r=RUN),
@@ -165,51 +172,63 @@ def tile_picked_wdime_silu_l_kernel(tc, x_words, x_scales, aT, w1, w3, w2, pos1,
             nc.sync.dma_start(out=out.rearrange("(m p) v -> p m v", p=P)[:, :, v0 : v0 + width], in_=result[:])
 
         LOW, HIGH, ALL = (0, 1), (2, 3), (0, 1, 2, 3)
-        g = {(half, d): sb.tile([P, PACK, HALF], F32, name="g%d%d" % (half, d)) for half in range(2) for d in range(2)}
-        for half, d in ((0, 0), (0, 1), (1, 0)):
+        a0 = quantise("a0", rounded("a0", a_raw[0], HALF, nc.vector.tensor_copy)[:], HALF)
+        g0 = [sb.tile([P, PACK, HALF], F32, name="g0%d" % d) for d in range(2)]
+        g10 = [sb.tile([P, 2, HALF], F32, name="g10%d" % b, tag=("a0_bf", "g101")[b], align_bytes=64) for b in range(2)]
+        g11 = sb.tile([P, PACK, HALF], F32, name="g11", tag="a0_raw", align_bytes=64)
+        gather(g11[:, 0, :], 0, 1, HALF, HALF, nc.vector)
+        gather(g10[0][:, 0, :], 0, 0, HALF, HALF, nc.vector)
+        for d in range(2):
             for t in range(PACK):
-                gather(g[half, d][:, t, :], t, d, half * HALF, HALF, nc.scalar)
+                gather(g0[d][:, t, :], t, d, 0, HALF, nc.scalar)
+        for t in range(1, PACK):
+            gather(g10[t // 2][:, t % 2, :], t, 0, HALF, HALF, nc.scalar)
         for blk in range(2):
-            for t in range(PACK):
-                gather(g[1, 1][:, t, blk * P : (blk + 1) * P], t, 1, HALF + blk * P, P, nc.scalar)
-        w3_bf = sb.tile([P, PACK * PASS], BF16, name="w3_bf", align_bytes=64)
+            for t in range(1, PACK):
+                gather(g11[:, t, blk * P : (blk + 1) * P], t, 1, HALF + blk * P, P, nc.scalar)
+
+        w3_bf = sb.tile([P, PACK * PASS], BF16, name="w3_bf", tag="xw1", align_bytes=64)
         nc.vector.tensor_copy(
             out=w3_bf[:].rearrange("p (t q r j) -> p t q j r", t=PACK, r=RUN, j=PACK),
             in_=w3_raw[:].rearrange("p j (q t r) -> p t q j r", t=PACK, r=RUN),
         )
+        a1_bf = rounded("a1", a_raw[1], HALF, nc.vector.tensor_copy, "xs")
         w3_codes, w3_scales = quantise("w3", w3_bf[:], H)
-        a0 = quantise("a0", rounded("a0", a_raw[0], HALF, nc.vector.tensor_copy)[:], HALF)
-        f00 = [filters(*a0, 0, HALF, LOW, "b4"), filters(*a0, 0, HALF, HIGH, "b5")]
-        p00 = sb.tile([P, PACK, HALF], F32, name="p00")
-        p01 = sb.tile([P, PACK, HALF], F32, name="p01")
-        p10 = sb.tile([P, PACK, HALF], F32, name="p10")
-        staged = rounded("a1", a_raw[1], HALF, nc.vector.tensor_copy, "w3_bf")
-        multiply(p00[:, 0:2, :], g[0, 0][:, 0:2, :], f00[0])
-        a1 = quantise("a1", staged[:], HALF)
-        f01 = [filters(*a1, 0, HALF, LOW, "b6"), filters(*a1, 0, HALF, HIGH, "b7")]
-        multiply(p00[:, 2:4, :], g[0, 0][:, 2:4, :], f00[1])
-        staged = rounded("a2", a_raw[2], HALF, nc.vector.tensor_copy, "w3_bf")
-        multiply(p01[:, 0:2, :], g[0, 1][:, 0:2, :], f01[0])
-        a2 = quantise("a2", staged[:], HALF)
+        f00 = [filters(*a0, 0, P, ALL, "b4"), filters(*a0, P, P, ALL, "b5")]
+        a1 = quantise("a1", a1_bf[:], HALF)
+        f01 = [filters(*a1, 0, P, ALL, "b6"), filters(*a1, P, P, ALL, "b7")]
+        p00 = [sb.tile([P, PASS], F32, name="p00%d" % c) for c in range(2)]
+        a2_bf = rounded("a2", a_raw[2], HALF, nc.vector.tensor_copy, "xw1")
+        multiply_woven(p00[0][:], g0[0][:, :, 0:P], f00[0])
+        a2 = quantise("a2", a2_bf[:], HALF)
         f10 = [filters(*a2, 0, HALF, LOW, "b0"), filters(*a2, 0, HALF, HIGH, "b1")]
-        multiply(p01[:, 2:4, :], g[0, 1][:, 2:4, :], f01[1])
-        staged = rounded("a3", a_raw[3], HALF, nc.vector.tensor_copy, "w3_bf")
-        z0 = sb.tile([P, HALF * PACK], BF16, name="z0", align_bytes=64)
-        add_and_round(z0[:], (p00[:], p01[:]))
-        a3 = quantise("a3", staged[:], HALF)
+        a3_bf = rounded("a3", a_raw[3], HALF, nc.vector.tensor_copy, "a2_raw")
+        multiply_woven(p00[1][:], g0[0][:, :, P:HALF], f00[1])
+        w2_bf = shared.tile([P, N * PACK], BF16, name="w2_bf", offset=2048, align_bytes=64)
+        nc.vector.tensor_copy(
+            out=w2_bf[:].rearrange("p (c r j) -> p c j r", r=RUN, j=PACK),
+            in_=w2_raw[:].rearrange("p j (c r) -> p c j r", r=RUN),
+        )
+        a3 = quantise("a3", a3_bf[:], HALF)
         f11 = [filters(*a3, 0, P, ALL, "b2"), filters(*a3, P, P, ALL, "b3")]
-        z0_q = quantise("z0", z0[:], HALF)
-        staged = rounded("w2", w2_raw, N, nc.vector.tensor_copy, "w3_bf")
-        multiply(p10[:, 0:2, :], g[1, 0][:, 0:2, :], f10[0])
-        w2_codes, w2_scales = quantise("w2", staged[:], N)
-        project("o0", z0_q[0], z0_q[1], 0, HALF, "b4")
-        multiply(p10[:, 2:4, :], g[1, 0][:, 2:4, :], f10[1])
-        p11 = [sb.tile([P, PACK, P], F32, name="p11_%d" % blk) for blk in range(2)]
+        p01 = sb.tile([P, 2, PASS], F32, name="p01", tag="w2_raw", align_bytes=64)
+        multiply_woven(p01[:, 0, :], g0[1][:, :, 0:P], f01[0])
+        w2_codes, w2_scales = quantise("w2", w2_bf[:], N)
+        multiply_woven(p01[:, 1, :], g0[1][:, :, P:HALF], f01[1])
+        z0 = shared.tile([P, HALF * PACK], BF16, name="z0", offset=1024, align_bytes=64)
+        for c in range(2):
+            nc.gpsimd.tensor_tensor(z0[:, c * PASS : (c + 1) * PASS], p00[c][:], p01[:, c, :], ADD)
+        p10 = shared.tile([P, PACK, HALF], F32, name="p10", offset=3072, align_bytes=64)
+        for b in range(2):
+            multiply(p10[:, 2 * b : 2 * b + 2, :], g10[b][:], f10[b])
+        p11 = [sb.tile([P, PACK, P], F32, name="p11_%d" % blk, tag=("a0_bf", "g101")[blk], align_bytes=64) for blk in range(2)]
         for blk in range(2):
-            multiply(p11[blk][:], g[1, 1][:, :, blk * P : (blk + 1) * P], f11[blk])
+            multiply(p11[blk][:], g11[:, :, blk * P : (blk + 1) * P], f11[blk])
+        z0_q = quantise("z0", z0[:], HALF)
+        project("o0", z0_q[0], z0_q[1], 0, HALF, "b4")
         z1 = [sb.tile([P, PASS], BF16, name="z1_%d" % blk, align_bytes=64) for blk in range(2)]
         for blk in range(2):
-            add_and_round(z1[blk][:], (p10[:, :, blk * P : (blk + 1) * P], p11[blk][:]))
+            add_and_round(z1[blk][:], (p10[:, :, blk * P : (blk + 1) * P], p11[blk][:]), nc.vector)
         for blk in range(2):
             codes, scales = quantise("z1_%d" % blk, z1[blk][:], P)
             project("o1_%d" % blk, codes, scales, HALF + blk * P, P, "b%d" % (5 + blk))

@@ -29,7 +29,6 @@ def tile_picked_wdime_silu_l_kernel(tc, x_words, x_scales, aT, w1, w3, w2, pos1,
     nc = tc.nc
     with ExitStack() as ctx:
         sb = ctx.enter_context(tc.tile_pool(name="sb", bufs=1))
-        shared = ctx.enter_context(tc.tile_pool(name="shared", bufs=1))
         ps = ctx.enter_context(tc.psum_pool(name="ps", bufs=1))
 
         def quantise(name, grouped, width, tag=None):
@@ -204,27 +203,23 @@ def tile_picked_wdime_silu_l_kernel(tc, x_words, x_scales, aT, w1, w3, w2, pos1,
         f10 = [filters(*a2, 0, HALF, LOW, "b0"), filters(*a2, 0, HALF, HIGH, "b1")]
         a3_bf = rounded("a3", a_raw[3], HALF, nc.vector.tensor_copy, "a2_raw")
         multiply_woven(p00[1][:], g0[0][:, :, P:HALF], f00[1])
-        w2_bf = shared.tile([P, N * PACK], BF16, name="w2_bf", offset=2048, align_bytes=64)
-        nc.vector.tensor_copy(
-            out=w2_bf[:].rearrange("p (c r j) -> p c j r", r=RUN, j=PACK),
-            in_=w2_raw[:].rearrange("p j (c r) -> p c j r", r=RUN),
-        )
         a3 = quantise("a3", a3_bf[:], HALF)
         f11 = [filters(*a3, 0, P, ALL, "b2"), filters(*a3, P, P, ALL, "b3")]
-        p01 = sb.tile([P, 2, PASS], F32, name="p01", tag="w2_raw", align_bytes=64)
-        multiply_woven(p01[:, 0, :], g0[1][:, :, 0:P], f01[0])
-        w2_codes, w2_scales = quantise("w2", w2_bf[:], N)
-        multiply_woven(p01[:, 1, :], g0[1][:, :, P:HALF], f01[1])
-        z0 = shared.tile([P, HALF * PACK], BF16, name="z0", offset=1024, align_bytes=64)
+        p01 = [sb.tile([P, PASS], F32, name="p01%d" % c, tag=("a3_raw", "p011")[c], align_bytes=64) for c in range(2)]
         for c in range(2):
-            nc.gpsimd.tensor_tensor(z0[:, c * PASS : (c + 1) * PASS], p00[c][:], p01[:, c, :], ADD)
-        p10 = shared.tile([P, PACK, HALF], F32, name="p10", offset=3072, align_bytes=64)
+            multiply_woven(p01[c][:], g0[1][:, :, c * P : (c + 1) * P], f01[c])
+        z0 = sb.tile([P, HALF * PACK], BF16, name="z0", tag="a2_raw", align_bytes=64)
+        for c in range(2):
+            nc.gpsimd.tensor_tensor(z0[:, c * PASS : (c + 1) * PASS], p00[c][:], p01[c][:], ADD)
+        p10 = sb.tile([P, PACK, HALF], F32, name="p10", tag="w3_raw", align_bytes=64)
         for b in range(2):
             multiply(p10[:, 2 * b : 2 * b + 2, :], g10[b][:], f10[b])
-        p11 = [sb.tile([P, PACK, P], F32, name="p11_%d" % blk, tag=("a0_bf", "g101")[blk], align_bytes=64) for blk in range(2)]
-        for blk in range(2):
-            multiply(p11[blk][:], g11[:, :, blk * P : (blk + 1) * P], f11[blk])
+        p11 = [sb.tile([P, PACK, P], F32, name="p11_%d" % blk, tag=("a0_bf", "w2_raw")[blk], align_bytes=64) for blk in range(2)]
+        multiply(p11[0][:], g11[:, :, 0:P], f11[0])
+        w2_bf = rounded("w2", w2_raw, N, nc.vector.tensor_copy, "g101")
         z0_q = quantise("z0", z0[:], HALF)
+        multiply(p11[1][:], g11[:, :, P:HALF], f11[1])
+        w2_codes, w2_scales = quantise("w2", w2_bf[:], N)
         project("o0", z0_q[0], z0_q[1], 0, HALF, "b4")
         z1 = [sb.tile([P, PASS], BF16, name="z1_%d" % blk, align_bytes=64) for blk in range(2)]
         for blk in range(2):

@@ -51,7 +51,7 @@ def tile_picked_wdime_silu_l_kernel(tc, x_words, x_scales, aT, w1, w3, w2, pos1,
             grouped = sb.tile([P, width * PACK], BF16, name=name + "_bf", tag=tag or name + "_bf", align_bytes=64)
             copy(
                 out=grouped[:].rearrange("p (c r j) -> p c j r", r=RUN, j=PACK),
-                in_=raw[:].rearrange("p j (c r) -> p c j r", r=RUN),
+                in_=raw.rearrange("p j (c r) -> p c j r", r=RUN),
             )
             return grouped
 
@@ -77,10 +77,10 @@ def tile_picked_wdime_silu_l_kernel(tc, x_words, x_scales, aT, w1, w3, w2, pos1,
             offsets = sb.tile([P, T // PER_COLUMN], U16, name="offsets%d" % d)
             nc.sync.dma_start(offsets[:], pos)
             lists.append(offsets)
-        pieces = [aT[:, d * T + half * HALF : d * T + (half + 1) * HALF] for half in range(2) for d in range(2)]
-        a_raw = [load_rows("a0", pieces[0])]
+        a_first = load_rows("a_first", aT[:, 0:HALF])
         w3_raw = load_rows("w3", w3)
-        a_raw.extend(load_rows("a%d" % n, pieces[n]) for n in range(1, 4))
+        a_list1 = load_rows("a_list1", aT[:, T : 2 * T])
+        a_last = load_rows("a_last", aT[:, HALF:T])
         w2_raw = sb.tile([P, PACK, N], F32, name="w2_raw", align_bytes=64)
         w2_rows = w2.rearrange("(q t r) n -> t q r n", t=PACK, r=4)
         for t in range(PACK):
@@ -126,8 +126,8 @@ def tile_picked_wdime_silu_l_kernel(tc, x_words, x_scales, aT, w1, w3, w2, pos1,
             for s, t in enumerate(planes):
                 nc.tensor.matmul_mx(
                     out=bank[:, s, :],
-                    lhsT=w3_codes[:, t * P : (t + 1) * P].bitcast(FP8X4),
-                    lhsT_scale=w3_scales[:, t * P : (t + 1) * P],
+                    lhsT=w3_q[t // 2][0][:, t % 2 * P : (t % 2 + 1) * P].bitcast(FP8X4),
+                    lhsT_scale=w3_q[t // 2][1][:, t % 2 * P : (t % 2 + 1) * P],
                     rhs=codes[:, c0 : c0 + width].bitcast(FP8X4),
                     rhs_scale=scales[:, c0 : c0 + width],
                     start=True,
@@ -171,59 +171,61 @@ def tile_picked_wdime_silu_l_kernel(tc, x_words, x_scales, aT, w1, w3, w2, pos1,
             nc.sync.dma_start(out=out.rearrange("(m p) v -> p m v", p=P)[:, :, v0 : v0 + width], in_=result[:])
 
         LOW, HIGH, ALL = (0, 1), (2, 3), (0, 1, 2, 3)
-        a0 = quantise("a0", rounded("a0", a_raw[0], HALF, nc.vector.tensor_copy)[:], HALF)
+        a0 = quantise("a0", rounded("a0", a_first[:], HALF, nc.vector.tensor_copy)[:], HALF)
         g0 = [sb.tile([P, PACK, HALF], F32, name="g0%d" % d) for d in range(2)]
-        g10 = [sb.tile([P, 2, HALF], F32, name="g10%d" % b, tag=("a0_bf", "g101")[b], align_bytes=64) for b in range(2)]
-        g11 = sb.tile([P, PACK, HALF], F32, name="g11", tag="a0_raw", align_bytes=64)
-        gather(g11[:, 0, :], 0, 1, HALF, HALF, nc.vector)
-        gather(g10[0][:, 0, :], 0, 0, HALF, HALF, nc.vector)
+        g11 = [sb.tile([P, 2, HALF], F32, name="g11%d" % b, tag=("a0_bf", "g111")[b], align_bytes=64) for b in range(2)]
+        g10 = sb.tile([P, PACK, HALF], F32, name="g10", tag="a_first_raw", align_bytes=64)
+        gather(g10[:, 0, :], 0, 0, HALF, HALF, nc.vector)
+        gather(g11[0][:, 0, :], 0, 1, HALF, HALF, nc.vector)
+        gather(g10[:, 1, :], 1, 0, HALF, HALF, nc.vector)
         for d in range(2):
             for t in range(PACK):
                 gather(g0[d][:, t, :], t, d, 0, HALF, nc.scalar)
         for t in range(1, PACK):
-            gather(g10[t // 2][:, t % 2, :], t, 0, HALF, HALF, nc.scalar)
+            gather(g11[t // 2][:, t % 2, :], t, 1, HALF, HALF, nc.scalar)
         for blk in range(2):
-            for t in range(1, PACK):
-                gather(g11[:, t, blk * P : (blk + 1) * P], t, 1, HALF + blk * P, P, nc.scalar)
+            for t in range(2, PACK):
+                gather(g10[:, t, blk * P : (blk + 1) * P], t, 0, HALF + blk * P, P, nc.scalar)
+        w2_bf = rounded("w2", w2_raw[:], N, nc.scalar.copy)
 
-        w3_bf = sb.tile([P, PACK * PASS], BF16, name="w3_bf", tag="xw1", align_bytes=64)
-        nc.vector.tensor_copy(
-            out=w3_bf[:].rearrange("p (t q r j) -> p t q j r", t=PACK, r=RUN, j=PACK),
-            in_=w3_raw[:].rearrange("p j (q t r) -> p t q j r", t=PACK, r=RUN),
-        )
-        a1_bf = rounded("a1", a_raw[1], HALF, nc.vector.tensor_copy, "xs")
-        w3_codes, w3_scales = quantise("w3", w3_bf[:], H)
+        w3_src = w3_raw[:].rearrange("p j (q t r) -> p t q j r", t=PACK, r=RUN)
+        w3_bf = [sb.tile([P, 2 * PASS], BF16, name="w3_bf%d" % b, align_bytes=64) for b in range(2)]
+        for b in range(2):
+            nc.vector.tensor_copy(
+                out=w3_bf[b][:].rearrange("p (t q r j) -> p t q j r", t=2, r=RUN, j=PACK), in_=w3_src[:, 2 * b : 2 * b + 2]
+            )
+        w3_q = [quantise("w3_%d" % b, w3_bf[b][:], 2 * P) for b in range(2)]
         f00 = [filters(*a0, 0, P, ALL, "b4"), filters(*a0, P, P, ALL, "b5")]
+        a1_bf = rounded("a1", a_list1[:, :, 0:HALF], HALF, nc.vector.tensor_copy)
+        a3_bf = rounded("a3", a_list1[:, :, HALF:T], HALF, nc.vector.tensor_copy)
         a1 = quantise("a1", a1_bf[:], HALF)
         f01 = [filters(*a1, 0, P, ALL, "b6"), filters(*a1, P, P, ALL, "b7")]
-        p00 = [sb.tile([P, PASS], F32, name="p00%d" % c) for c in range(2)]
-        a2_bf = rounded("a2", a_raw[2], HALF, nc.vector.tensor_copy, "xw1")
-        multiply_woven(p00[0][:], g0[0][:, :, 0:P], f00[0])
-        a2 = quantise("a2", a2_bf[:], HALF)
-        f10 = [filters(*a2, 0, HALF, LOW, "b0"), filters(*a2, 0, HALF, HIGH, "b1")]
-        a3_bf = rounded("a3", a_raw[3], HALF, nc.vector.tensor_copy, "a2_raw")
-        multiply_woven(p00[1][:], g0[0][:, :, P:HALF], f00[1])
+        p00 = sb.tile([P, 2, PASS], F32, name="p00", tag="a_list1_raw", align_bytes=64)
+        multiply_woven(p00[:, 0, :], g0[0][:, :, 0:P], f00[0])
         a3 = quantise("a3", a3_bf[:], HALF)
-        f11 = [filters(*a3, 0, P, ALL, "b2"), filters(*a3, P, P, ALL, "b3")]
-        p01 = [sb.tile([P, PASS], F32, name="p01%d" % c, tag=("a3_raw", "p011")[c], align_bytes=64) for c in range(2)]
+        f11 = [filters(*a3, 0, HALF, LOW, "b0"), filters(*a3, 0, HALF, HIGH, "b1")]
+        multiply_woven(p00[:, 1, :], g0[0][:, :, P:HALF], f00[1])
+        a2_bf = [rounded("a2_%d" % c, a_last[:, :, c * P : (c + 1) * P], P, nc.vector.tensor_copy) for c in range(2)]
+        f10 = [filters(*quantise("a2_%d" % c, a2_bf[c][:], P), 0, P, ALL, ("b2", "b3")[c]) for c in range(2)]
+        p01 = sb.tile([P, 2, PASS], F32, name="p01", tag="a_last_raw", align_bytes=64)
+        z0 = sb.tile([P, HALF * PACK], BF16, name="z0", align_bytes=64)
         for c in range(2):
-            multiply_woven(p01[c][:], g0[1][:, :, c * P : (c + 1) * P], f01[c])
-        z0 = sb.tile([P, HALF * PACK], BF16, name="z0", tag="a2_raw", align_bytes=64)
-        for c in range(2):
-            nc.gpsimd.tensor_tensor(z0[:, c * PASS : (c + 1) * PASS], p00[c][:], p01[c][:], ADD)
-        p10 = sb.tile([P, PACK, HALF], F32, name="p10", tag="w3_raw", align_bytes=64)
+            multiply_woven(p01[:, c, :], g0[1][:, :, c * P : (c + 1) * P], f01[c])
+            nc.gpsimd.tensor_tensor(z0[:, c * PASS : (c + 1) * PASS], p00[:, c, :], p01[:, c, :], ADD)
+        p11 = sb.tile([P, PACK, HALF], F32, name="p11", tag="a2_0_bf", align_bytes=64)
         for b in range(2):
-            multiply(p10[:, 2 * b : 2 * b + 2, :], g10[b][:], f10[b])
-        p11 = [sb.tile([P, PACK, P], F32, name="p11_%d" % blk, tag=("a0_bf", "w2_raw")[blk], align_bytes=64) for blk in range(2)]
-        multiply(p11[0][:], g11[:, :, 0:P], f11[0])
-        w2_bf = rounded("w2", w2_raw, N, nc.vector.tensor_copy, "g101")
-        z0_q = quantise("z0", z0[:], HALF)
-        multiply(p11[1][:], g11[:, :, P:HALF], f11[1])
+            multiply(p11[:, 2 * b : 2 * b + 2, :], g11[b][:], f11[b])
+        p10 = [sb.tile([P, PACK, P], F32, name="p10_%d" % blk, tag=("a0_bf", "g111")[blk], align_bytes=64) for blk in range(2)]
+        multiply(p10[0][:], g10[:, :, 0:P], f10[0])
+
+        multiply(p10[1][:], g10[:, :, P:HALF], f10[1])
         w2_codes, w2_scales = quantise("w2", w2_bf[:], N)
+        z0_q = quantise("z0", z0[:], HALF)
         project("o0", z0_q[0], z0_q[1], 0, HALF, "b4")
-        z1 = [sb.tile([P, PASS], BF16, name="z1_%d" % blk, align_bytes=64) for blk in range(2)]
-        for blk in range(2):
-            add_and_round(z1[blk][:], (p10[:, :, blk * P : (blk + 1) * P], p11[blk][:]), nc.vector)
+        z1 = [sb.tile([P, PASS], BF16, name="z1_%d" % blk, tag=("w2_bf", "z0")[blk], align_bytes=64) for blk in range(2)]
+        add_and_round(z1[0][:], (p10[0][:], p11[:, :, 0:P]), nc.vector)
+
+        add_and_round(z1[1][:], (p10[1][:], p11[:, :, P:HALF]), nc.vector)
         for blk in range(2):
             codes, scales = quantise("z1_%d" % blk, z1[blk][:], P)
             project("o1_%d" % blk, codes, scales, HALF + blk * P, P, "b%d" % (5 + blk))

@@ -20,7 +20,7 @@ ADD = mybir.AluOpType.add
 P = 128
 PACK = 4
 PASS = P * PACK
-RUN = 4
+RUN = 2
 HALF = T // 2
 PER_COLUMN = 16
 
@@ -82,7 +82,7 @@ def tile_picked_wdime_silu_l_kernel(tc, x_words, x_scales, aT, w1, w3, w2, pos1,
         a_list1 = load_rows("a_list1", aT[:, T : 2 * T])
         a_last = load_rows("a_last", aT[:, HALF:T])
         w2_raw = sb.tile([P, PACK, N], F32, name="w2_raw", align_bytes=64)
-        w2_rows = w2.rearrange("(q t r) n -> t q r n", t=PACK, r=4)
+        w2_rows = w2.rearrange("(q t r) n -> t q r n", t=PACK, r=RUN)
         for t in range(PACK):
             nc.sync.dma_start(out=w2_raw[:, t, :], in_=w2_rows[t])
 
@@ -140,9 +140,9 @@ def tile_picked_wdime_silu_l_kernel(tc, x_words, x_scales, aT, w1, w3, w2, pos1,
 
         def multiply_woven(product, picked, bank):
             nc.vector.tensor_tensor(
-                product.rearrange("p (c r t) -> p c t r", r=4, t=PACK),
-                picked.rearrange("p t (c r) -> p c t r", r=4),
-                bank[:].rearrange("p t (c r) -> p c t r", r=4),
+                product.rearrange("p (c r t) -> p c t r", r=RUN, t=PACK),
+                picked.rearrange("p t (c r) -> p c t r", r=RUN),
+                bank[:].rearrange("p t (c r) -> p c t r", r=RUN),
                 MULT,
             )
 
@@ -183,9 +183,8 @@ def tile_picked_wdime_silu_l_kernel(tc, x_words, x_scales, aT, w1, w3, w2, pos1,
                 gather(g0[d][:, t, :], t, d, 0, HALF, nc.scalar)
         for t in range(1, PACK):
             gather(g11[t // 2][:, t % 2, :], t, 1, HALF, HALF, nc.scalar)
-        for blk in range(2):
-            for t in range(2, PACK):
-                gather(g10[:, t, blk * P : (blk + 1) * P], t, 0, HALF + blk * P, P, nc.scalar)
+        for t in range(2, PACK):
+            gather(g10[:, t, :], t, 0, HALF, HALF, nc.scalar)
         w2_bf = rounded("w2", w2_raw[:], N, nc.scalar.copy)
 
         w3_src = w3_raw[:].rearrange("p j (q t r) -> p t q j r", t=PACK, r=RUN)

@@ -29,6 +29,7 @@ def tile_picked_wdime_silu_l_kernel(tc, x_words, x_scales, aT, w1, w3, w2, pos1,
     nc = tc.nc
     with ExitStack() as ctx:
         sb = ctx.enter_context(tc.tile_pool(name="sb", bufs=1))
+        shared = ctx.enter_context(tc.tile_pool(name="shared", bufs=1))
         ps = ctx.enter_context(tc.psum_pool(name="ps", bufs=1))
 
         def quantise(name, grouped, width, tag=None):
@@ -77,8 +78,10 @@ def tile_picked_wdime_silu_l_kernel(tc, x_words, x_scales, aT, w1, w3, w2, pos1,
             offsets = sb.tile([P, T // PER_COLUMN], U16, name="offsets%d" % d)
             nc.sync.dma_start(offsets[:], pos)
             lists.append(offsets)
-        a_first = load_rows("a_first", aT[:, 0:HALF])
-        w3_raw = load_rows("w3", w3)
+        a_first = shared.tile([P, PACK, HALF], F32, name="a_first", offset=0, align_bytes=64)
+        nc.sync.dma_start(out=a_first[:], in_=aT[:, 0:HALF].rearrange("(p j) c -> p j c", j=PACK))
+        w3_raw = shared.tile([P, PACK, H], F32, name="w3_raw", offset=8192, align_bytes=64)
+        nc.sync.dma_start(out=w3_raw[:], in_=w3.rearrange("(p j) c -> p j c", j=PACK))
         a_list1 = load_rows("a_list1", aT[:, T : 2 * T])
         a_last = load_rows("a_last", aT[:, HALF:T])
         w2_raw = sb.tile([P, PACK, N], F32, name="w2_raw", align_bytes=64)
@@ -90,11 +93,24 @@ def tile_picked_wdime_silu_l_kernel(tc, x_words, x_scales, aT, w1, w3, w2, pos1,
         w1_q = []
         for g in range(2):
             src = w1_raw[g][:].rearrange("p j (q t r) -> p t q j r", t=PACK, r=RUN)
-            for t in range(PACK):
-                grouped = sb.tile([P, PASS], BF16, name="w1_%d_bf%d" % (g, t), align_bytes=64)
-                rounds = nc.scalar.copy if t % 2 else nc.vector.tensor_copy
-                rounds(out=grouped[:].rearrange("p (q r j) -> p q j r", r=RUN, j=PACK), in_=src[:, t])
-                w1_q.append(quantise("w1_%d_%d" % (g, t), grouped[:], P))
+            grouped = [sb.tile([P, PASS], BF16, name="w1_%d_bf%d" % (g, t), align_bytes=64) for t in range(PACK - 1)]
+
+            def round_plane(t, q0, q1, copy):
+                copy(out=grouped[t][:].rearrange("p (q r j) -> p q j r", r=RUN, j=PACK)[:, q0:q1], in_=src[:, t, q0:q1])
+
+            pairs = P // RUN
+            round_plane(0, 0, pairs // 2, nc.vector.tensor_copy)
+            round_plane(0, pairs // 2, pairs, nc.scalar.copy)
+            round_plane(1, 0, pairs, nc.scalar.copy)
+            round_plane(2, 0, pairs, nc.vector.tensor_copy)
+            planes = {t: quantise("w1_%d_%d" % (g, t), grouped[t][:], P) for t in (0, 2)}
+            grouped.append(sb.tile([P, PASS], BF16, name="w1_%d_bf3" % g, tag="w1_%d_bf0" % g, align_bytes=64))
+            round_plane(3, 0, pairs // 2, nc.vector.tensor_copy)
+            round_plane(3, pairs // 2, pairs, nc.scalar.copy)
+            for t in (1, 3):
+                planes[t] = quantise("w1_%d_%d" % (g, t), grouped[t][:], P)
+            w1_q += [planes[t] for t in range(PACK)]
+        h = [sb.tile([P, T], F32, name="h%d" % t, align_bytes=64) for t in range(PACK)]
         for g in range(2):
             for t in range(PACK):
                 codes, scales = w1_q[PACK * g + t]
@@ -107,12 +123,8 @@ def tile_picked_wdime_silu_l_kernel(tc, x_words, x_scales, aT, w1, w3, w2, pos1,
                     start=(g == 0),
                     stop=(g == 1),
                 )
-
-        h = []
         for t in range(PACK):
-            plane = sb.tile([P, T], F32, name="h%d" % t, align_bytes=64)
-            nc.scalar.activation(plane[:], h_banks[t][:], SILU)
-            h.append(plane)
+            nc.scalar.activation(h[t][:], h_banks[t][:], SILU)
 
         def gather(picked, t, d, v0, width, engine):
             window = h[t][:].indirect(lists[d][:, v0 // PER_COLUMN : (v0 + width) // PER_COLUMN])
@@ -121,37 +133,36 @@ def tile_picked_wdime_silu_l_kernel(tc, x_words, x_scales, aT, w1, w3, w2, pos1,
             else:
                 nc.scalar.activation(picked, window, COPY)
 
-        def filters(codes, scales, c0, width, planes, tag):
-            bank = ps.tile([P, len(planes), width], F32, name="f_bank", tag=tag)
-            for s, t in enumerate(planes):
+        def round_into(grouped, raw, copy):
+            copy(
+                out=grouped.rearrange("p (c r j) -> p c j r", r=RUN, j=PACK),
+                in_=raw.rearrange("p j (c r) -> p c j r", r=RUN),
+            )
+
+        def quantise_into(codes, scales, grouped):
+            nc.vector.quantize_mx(out=codes.bitcast(FP8X4), scales=scales, in_=grouped)
+            return codes, scales
+
+        def filters(codes, scales, c0, tag):
+            bank = ps.tile([P, PACK, P], F32, name="f_bank", tag=tag)
+            for t in range(PACK):
                 nc.tensor.matmul_mx(
-                    out=bank[:, s, :],
+                    out=bank[:, t, :],
                     lhsT=w3_q[t // 2][0][:, t % 2 * P : (t % 2 + 1) * P].bitcast(FP8X4),
                     lhsT_scale=w3_q[t // 2][1][:, t % 2 * P : (t % 2 + 1) * P],
-                    rhs=codes[:, c0 : c0 + width].bitcast(FP8X4),
-                    rhs_scale=scales[:, c0 : c0 + width],
+                    rhs=codes[:, c0 : c0 + P].bitcast(FP8X4),
+                    rhs_scale=scales[:, c0 : c0 + P],
                     start=True,
                     stop=True,
                 )
             return bank
 
         def multiply(product, picked, bank):
-            nc.vector.tensor_tensor(product, picked, bank[:], MULT)
-
-        def multiply_woven(product, picked, bank):
             nc.vector.tensor_tensor(
                 product.rearrange("p (c r t) -> p c t r", r=RUN, t=PACK),
                 picked.rearrange("p t (c r) -> p c t r", r=RUN),
                 bank[:].rearrange("p t (c r) -> p c t r", r=RUN),
                 MULT,
-            )
-
-        def add_and_round(z, terms, engine):
-            engine.tensor_tensor(
-                z.rearrange("p (c r t) -> p c t r", r=RUN, t=PACK),
-                terms[0].rearrange("p t (c r) -> p c t r", r=RUN),
-                terms[1].rearrange("p t (c r) -> p c t r", r=RUN),
-                ADD,
             )
 
         def project(name, codes, scales, v0, width, tag):
@@ -161,8 +172,8 @@ def tile_picked_wdime_silu_l_kernel(tc, x_words, x_scales, aT, w1, w3, w2, pos1,
                     out=bank[:, m, :],
                     lhsT=w2_codes[:, m * P : (m + 1) * P].bitcast(FP8X4),
                     lhsT_scale=w2_scales[:, m * P : (m + 1) * P],
-                    rhs=codes[:].bitcast(FP8X4),
-                    rhs_scale=scales[:],
+                    rhs=codes.bitcast(FP8X4),
+                    rhs_scale=scales,
                     start=True,
                     stop=True,
                 )
@@ -170,22 +181,18 @@ def tile_picked_wdime_silu_l_kernel(tc, x_words, x_scales, aT, w1, w3, w2, pos1,
             nc.scalar.activation(result[:], bank[:], SILU)
             nc.sync.dma_start(out=out.rearrange("(m p) v -> p m v", p=P)[:, :, v0 : v0 + width], in_=result[:])
 
-        LOW, HIGH, ALL = (0, 1), (2, 3), (0, 1, 2, 3)
         a0 = quantise("a0", rounded("a0", a_first[:], HALF, nc.vector.tensor_copy)[:], HALF)
-        g0 = [sb.tile([P, PACK, HALF], F32, name="g0%d" % d) for d in range(2)]
-        g11 = [sb.tile([P, 2, HALF], F32, name="g11%d" % b, tag=("a0_bf", "g111")[b], align_bytes=64) for b in range(2)]
-        g10 = sb.tile([P, PACK, HALF], F32, name="g10", tag="a_first_raw", align_bytes=64)
-        gather(g10[:, 0, :], 0, 0, HALF, HALF, nc.vector)
-        gather(g11[0][:, 0, :], 0, 1, HALF, HALF, nc.vector)
-        gather(g10[:, 1, :], 1, 0, HALF, HALF, nc.vector)
+        early = [
+            shared.tile([P, PACK, HALF], F32, name="early0", offset=0, align_bytes=64),
+            sb.tile([P, PACK, HALF], F32, name="early1", tag="a0_bf", align_bytes=64),
+        ]
+        on_vector = ((0, 0), (0, 1), (1, 0))
+        for t, d in on_vector:
+            gather(early[d][:, t, :], t, d, 0, HALF, nc.vector)
         for d in range(2):
             for t in range(PACK):
-                gather(g0[d][:, t, :], t, d, 0, HALF, nc.scalar)
-        for t in range(1, PACK):
-            gather(g11[t // 2][:, t % 2, :], t, 1, HALF, HALF, nc.scalar)
-        for t in range(2, PACK):
-            gather(g10[:, t, :], t, 0, HALF, HALF, nc.scalar)
-        w2_bf = rounded("w2", w2_raw[:], N, nc.scalar.copy)
+                if (t, d) not in on_vector:
+                    gather(early[d][:, t, :], t, d, 0, HALF, nc.scalar)
 
         w3_src = w3_raw[:].rearrange("p j (q t r) -> p t q j r", t=PACK, r=RUN)
         w3_bf = [sb.tile([P, 2 * PASS], BF16, name="w3_bf%d" % b, align_bytes=64) for b in range(2)]
@@ -193,38 +200,62 @@ def tile_picked_wdime_silu_l_kernel(tc, x_words, x_scales, aT, w1, w3, w2, pos1,
             nc.vector.tensor_copy(
                 out=w3_bf[b][:].rearrange("p (t q r j) -> p t q j r", t=2, r=RUN, j=PACK), in_=w3_src[:, 2 * b : 2 * b + 2]
             )
-        w3_q = [quantise("w3_%d" % b, w3_bf[b][:], 2 * P) for b in range(2)]
-        f00 = [filters(*a0, 0, P, ALL, "b4"), filters(*a0, P, P, ALL, "b5")]
-        a1_bf = rounded("a1", a_list1[:, :, 0:HALF], HALF, nc.vector.tensor_copy)
-        a3_bf = rounded("a3", a_list1[:, :, HALF:T], HALF, nc.vector.tensor_copy)
-        a1 = quantise("a1", a1_bf[:], HALF)
-        f01 = [filters(*a1, 0, P, ALL, "b6"), filters(*a1, P, P, ALL, "b7")]
-        p00 = sb.tile([P, 2, PASS], F32, name="p00", tag="a_list1_raw", align_bytes=64)
-        multiply_woven(p00[:, 0, :], g0[0][:, :, 0:P], f00[0])
-        a3 = quantise("a3", a3_bf[:], HALF)
-        f11 = [filters(*a3, 0, HALF, LOW, "b0"), filters(*a3, 0, HALF, HIGH, "b1")]
-        multiply_woven(p00[:, 1, :], g0[0][:, :, P:HALF], f00[1])
-        a2_bf = [rounded("a2_%d" % c, a_last[:, :, c * P : (c + 1) * P], P, nc.vector.tensor_copy) for c in range(2)]
-        f10 = [filters(*quantise("a2_%d" % c, a2_bf[c][:], P), 0, P, ALL, ("b2", "b3")[c]) for c in range(2)]
-        p01 = sb.tile([P, 2, PASS], F32, name="p01", tag="a_last_raw", align_bytes=64)
-        z0 = sb.tile([P, HALF * PACK], BF16, name="z0", align_bytes=64)
+        late = [shared.tile([P, PACK, HALF], F32, name="late%d" % d, offset=8192 + 4096 * d, align_bytes=64) for d in range(2)]
+        for t in range(PACK):
+            gather(late[1][:, t, :], t, 1, HALF, HALF, nc.scalar)
         for c in range(2):
-            multiply_woven(p01[:, c, :], g0[1][:, :, c * P : (c + 1) * P], f01[c])
-            nc.gpsimd.tensor_tensor(z0[:, c * PASS : (c + 1) * PASS], p00[:, c, :], p01[:, c, :], ADD)
-        p11 = sb.tile([P, PACK, HALF], F32, name="p11", tag="a2_0_bf", align_bytes=64)
-        for b in range(2):
-            multiply(p11[:, 2 * b : 2 * b + 2, :], g11[b][:], f11[b])
-        p10 = [sb.tile([P, PACK, P], F32, name="p10_%d" % blk, tag=("a0_bf", "g111")[blk], align_bytes=64) for blk in range(2)]
-        multiply(p10[0][:], g10[:, :, 0:P], f10[0])
+            for t in range(PACK):
+                gather(late[0][:, t, c * P : (c + 1) * P], t, 0, HALF + c * P, P, nc.scalar)
+        w2_bf = rounded("w2", w2_raw[:], N, nc.scalar.copy)
+        w3_q = [quantise("w3_%d" % b, w3_bf[b][:], 2 * P) for b in range(2)]
+        f0 = [filters(*a0, 0, "b4"), filters(*a0, P, "b5")]
+        a1_bf = shared.tile([P, HALF * PACK], BF16, name="a1_bf", offset=16384 + 1024, align_bytes=64)
+        round_into(a1_bf[:], a_list1[:, :, 0:HALF], nc.vector.tensor_copy)
+        a3_bf = shared.tile([P, HALF * PACK], BF16, name="a3_bf", offset=24576, align_bytes=64)
+        round_into(a3_bf[:], a_list1[:, :, HALF:T], nc.vector.tensor_copy)
+        a1 = quantise("a1", a1_bf[:], HALF)
+        f1 = [filters(*a1, 0, "b6"), filters(*a1, P, "b7")]
+        a3 = quantise("a3", a3_bf[:], HALF)
+        f1 += [filters(*a3, 0, "b0"), filters(*a3, P, "b1")]
+        a2_bf = shared.tile([P, HALF * PACK], BF16, name="a2_bf", offset=24576, align_bytes=64)
+        nc.gpsimd.tensor_scalar(
+            a2_bf[:].rearrange("p (c j) -> p c j", j=PACK), a_last[:].rearrange("p j c -> p c j"), 1.0, 0.0, MULT, ADD
+        )
 
-        multiply(p10[1][:], g10[:, :, P:HALF], f10[1])
+        p0 = [
+            shared.tile([P, PASS], F32, name="p0_0", offset=16384, align_bytes=64),
+            shared.tile([P, PASS], F32, name="p0_1", offset=16384 + 2048, align_bytes=64),
+            sb.tile([P, PASS], F32, name="p0_2", align_bytes=64),
+            sb.tile([P, PASS], F32, name="p0_3", align_bytes=64),
+        ]
+        p1 = [
+            sb.tile([P, PASS], F32, name="p1_0", align_bytes=64),
+            sb.tile([P, PASS], F32, name="p1_1", align_bytes=64),
+            shared.tile([P, PASS], F32, name="p1_2", offset=24576 - 2048 + 64, align_bytes=64),
+            sb.tile([P, PASS], F32, name="p1_3", tag="a0_bf", align_bytes=64),
+        ]
+        multiply(p0[0][:], early[0][:, :, 0:P], f0[0])
+        multiply(p0[1][:], early[0][:, :, P:HALF], f0[1])
+        multiply(p1[0][:], early[1][:, :, 0:P], f1[0])
+        a2_codes = shared.tile([P, HALF], U32, name="a2_codes", offset=0, align_bytes=64)
+        a2_scales = sb.tile([P, HALF], U8, name="a2_scales", align_bytes=64)
+        a2 = quantise_into(a2_codes[:], a2_scales[:], a2_bf[:])
+        f0 += [filters(*a2, 0, "b2"), filters(*a2, P, "b3")]
+        z_first = shared.tile([P, 2 * PASS], BF16, name="z_first", offset=24576 + 64, align_bytes=64)
+        nc.gpsimd.tensor_tensor(z_first[:, 0:PASS], p0[0][:], p1[0][:], ADD)
+        multiply(p1[1][:], early[1][:, :, P:HALF], f1[1])
+        nc.gpsimd.tensor_tensor(z_first[:, PASS : 2 * PASS], p0[1][:], p1[1][:], ADD)
+        multiply(p1[2][:], late[1][:, :, 0:P], f1[2])
+        multiply(p1[3][:], late[1][:, :, P:HALF], f1[3])
+        multiply(p0[2][:], late[0][:, :, 0:P], f0[2])
+        multiply(p0[3][:], late[0][:, :, P:HALF], f0[3])
+        zf = quantise("zf", z_first[:], HALF)
+        z = [sb.tile([P, PASS], BF16, name="z%d" % c, tag=("z0", "w2_bf")[c], align_bytes=64) for c in range(2)]
+        nc.vector.tensor_tensor(z[0][:], p0[2][:], p1[2][:], ADD)
         w2_codes, w2_scales = quantise("w2", w2_bf[:], N)
-        z0_q = quantise("z0", z0[:], HALF)
-        project("o0", z0_q[0], z0_q[1], 0, HALF, "b4")
-        z1 = [sb.tile([P, PASS], BF16, name="z1_%d" % blk, tag=("w2_bf", "z0")[blk], align_bytes=64) for blk in range(2)]
-        add_and_round(z1[0][:], (p10[0][:], p11[:, :, 0:P]), nc.vector)
-
-        add_and_round(z1[1][:], (p10[1][:], p11[:, :, P:HALF]), nc.vector)
-        for blk in range(2):
-            codes, scales = quantise("z1_%d" % blk, z1[blk][:], P)
-            project("o1_%d" % blk, codes, scales, HALF + blk * P, P, "b%d" % (5 + blk))
+        project("o0", zf[0][:], zf[1][:], 0, HALF, "b4")
+        codes, scales = quantise("z1_0", z[0][:], P)
+        project("o1_0", codes[:], scales[:], HALF, P, "b5")
+        nc.vector.tensor_tensor(z[1][:], p0[3][:], p1[3][:], ADD)
+        codes, scales = quantise("z1_1", z[1][:], P)
+        project("o1_1", codes[:], scales[:], HALF + P, P, "b6")

@@ -181,7 +181,14 @@ def tile_picked_wdime_silu_l_kernel(tc, x_words, x_scales, aT, w1, w3, w2, pos1,
             nc.scalar.activation(result[:], bank[:], SILU)
             nc.sync.dma_start(out=out.rearrange("(m p) v -> p m v", p=P)[:, :, v0 : v0 + width], in_=result[:])
 
-        a0 = quantise("a0", rounded("a0", a_first[:], HALF, nc.vector.tensor_copy)[:], HALF)
+        a0_bf = sb.tile([P, HALF * PACK], BF16, name="a0_bf", align_bytes=64)
+        for c in range(2):
+            round_into(a0_bf[:, c * PASS : (c + 1) * PASS], a_first[:, :, c * P : (c + 1) * P], nc.vector.tensor_copy)
+        a0_codes = sb.tile([P, HALF], U32, name="a0_codes", align_bytes=64)
+        a0_scales = sb.tile([P, HALF], U8, name="a0_scales", align_bytes=64)
+        for c in range(2):
+            quantise_into(a0_codes[:, c * P : (c + 1) * P], a0_scales[:, c * P : (c + 1) * P], a0_bf[:, c * PASS : (c + 1) * PASS])
+        a0 = a0_codes, a0_scales
         early = [
             shared.tile([P, PACK, HALF], F32, name="early0", offset=0, align_bytes=64),
             sb.tile([P, PACK, HALF], F32, name="early1", tag="a0_bf", align_bytes=64),
@@ -203,9 +210,10 @@ def tile_picked_wdime_silu_l_kernel(tc, x_words, x_scales, aT, w1, w3, w2, pos1,
         late = [shared.tile([P, PACK, HALF], F32, name="late%d" % d, offset=8192 + 4096 * d, align_bytes=64) for d in range(2)]
         for t in range(PACK):
             gather(late[1][:, t, :], t, 1, HALF, HALF, nc.scalar)
+        for t in range(PACK - 1):
+            gather(late[0][:, t, :], t, 0, HALF, HALF, nc.scalar)
         for c in range(2):
-            for t in range(PACK):
-                gather(late[0][:, t, c * P : (c + 1) * P], t, 0, HALF + c * P, P, nc.scalar)
+            gather(late[0][:, PACK - 1, c * P : (c + 1) * P], PACK - 1, 0, HALF + c * P, P, nc.scalar)
         w2_bf = rounded("w2", w2_raw[:], N, nc.scalar.copy)
         w3_q = [quantise("w3_%d" % b, w3_bf[b][:], 2 * P) for b in range(2)]
         f0 = [filters(*a0, 0, "b4"), filters(*a0, P, "b5")]
@@ -250,12 +258,11 @@ def tile_picked_wdime_silu_l_kernel(tc, x_words, x_scales, aT, w1, w3, w2, pos1,
         multiply(p0[2][:], late[0][:, :, 0:P], f0[2])
         multiply(p0[3][:], late[0][:, :, P:HALF], f0[3])
         zf = quantise("zf", z_first[:], HALF)
-        z = [sb.tile([P, PASS], BF16, name="z%d" % c, tag=("z0", "w2_bf")[c], align_bytes=64) for c in range(2)]
-        nc.vector.tensor_tensor(z[0][:], p0[2][:], p1[2][:], ADD)
         w2_codes, w2_scales = quantise("w2", w2_bf[:], N)
         project("o0", zf[0][:], zf[1][:], 0, HALF, "b4")
-        codes, scales = quantise("z1_0", z[0][:], P)
-        project("o1_0", codes[:], scales[:], HALF, P, "b5")
-        nc.vector.tensor_tensor(z[1][:], p0[3][:], p1[3][:], ADD)
-        codes, scales = quantise("z1_1", z[1][:], P)
-        project("o1_1", codes[:], scales[:], HALF + P, P, "b6")
+        z = [sb.tile([P, PASS], BF16, name="z%d" % c, tag=("w2_raw", "w2_bf")[c], align_bytes=64) for c in range(2)]
+        for c in range(2):
+            nc.vector.tensor_tensor(z[c][:], p0[2 + c][:], p1[2 + c][:], ADD)
+        for c in range(2):
+            codes, scales = quantise("z1_%d" % c, z[c][:], P)
+            project("o1_%d" % c, codes[:], scales[:], HALF + c * P, P, "b%d" % (5 + c))

@@ -165,11 +165,11 @@ def tile_picked_wdime_silu_l_kernel(tc, x_words, x_scales, aT, w1, w3, w2, pos1,
                 MULT,
             )
 
-        def project(name, codes, scales, v0, width, tag):
-            bank = ps.tile([P, 2, width], F32, name=name + "_bank", tag=tag)
+        def project(name, codes, scales, v0, width, tags):
+            banks = {tag: ps.tile([P, tags.count(tag), width], F32, name=name + tag, tag=tag) for tag in sorted(set(tags))}
             for m in range(N // P):
                 nc.tensor.matmul_mx(
-                    out=bank[:, m, :],
+                    out=banks[tags[m]][:, m - tags.index(tags[m]), :],
                     lhsT=w2_codes[:, m * P : (m + 1) * P].bitcast(FP8X4),
                     lhsT_scale=w2_scales[:, m * P : (m + 1) * P],
                     rhs=codes.bitcast(FP8X4),
@@ -177,9 +177,12 @@ def tile_picked_wdime_silu_l_kernel(tc, x_words, x_scales, aT, w1, w3, w2, pos1,
                     start=True,
                     stop=True,
                 )
-            result = sb.tile([P, 2, width], F32, name=name + "_o")
-            nc.scalar.activation(result[:], bank[:], SILU)
-            nc.sync.dma_start(out=out.rearrange("(m p) v -> p m v", p=P)[:, :, v0 : v0 + width], in_=result[:])
+            rows = out.rearrange("(m p) v -> p m v", p=P)
+            for tag, bank in banks.items():
+                m0, m1 = tags.index(tag), tags.index(tag) + tags.count(tag)
+                result = sb.tile([P, m1 - m0, width], F32, name=name + tag + "_o")
+                nc.scalar.activation(result[:], bank[:], SILU)
+                nc.sync.dma_start(out=rows[:, m0:m1, v0 : v0 + width], in_=result[:])
 
         a0_bf = sb.tile([P, HALF * PACK], BF16, name="a0_bf", align_bytes=64)
         for c in range(2):
@@ -259,10 +262,12 @@ def tile_picked_wdime_silu_l_kernel(tc, x_words, x_scales, aT, w1, w3, w2, pos1,
         multiply(p0[3][:], late[0][:, :, P:HALF], f0[3])
         zf = quantise("zf", z_first[:], HALF)
         w2_codes, w2_scales = quantise("w2", w2_bf[:], N)
-        project("o0", zf[0][:], zf[1][:], 0, HALF, "b4")
+        project("o0", zf[0][:], zf[1][:], 0, HALF, ("b4", "b5"))
         z = [sb.tile([P, PASS], BF16, name="z%d" % c, tag=("w2_raw", "w2_bf")[c], align_bytes=64) for c in range(2)]
-        for c in range(2):
-            nc.vector.tensor_tensor(z[c][:], p0[2 + c][:], p1[2 + c][:], ADD)
-        for c in range(2):
-            codes, scales = quantise("z1_%d" % c, z[c][:], P)
-            project("o1_%d" % c, codes[:], scales[:], HALF + c * P, P, "b%d" % (5 + c))
+        nc.vector.tensor_tensor(z[0][:], p0[2][:], p1[2][:], ADD)
+        nc.vector.tensor_tensor(z[1][:, 0:HALF], p0[3][:, 0:HALF], p1[3][:, 0:HALF], ADD)
+        codes, scales = quantise("z2", z[0][:], P)
+        project("o1", codes[:], scales[:], HALF, P, ("b6", "b6"))
+        nc.vector.tensor_tensor(z[1][:, HALF:PASS], p0[3][:, HALF:PASS], p1[3][:, HALF:PASS], ADD)
+        codes, scales = quantise("z3", z[1][:], P)
+        project("o2", codes[:], scales[:], HALF + P, P, ("b7", "b0"))

@@ -196,13 +196,13 @@ def tile_picked_wdime_silu_l_kernel(tc, x_words, x_scales, aT, w1, w3, w2, pos1,
             shared.tile([P, PACK, HALF], F32, name="early0", offset=0, align_bytes=64),
             sb.tile([P, PACK, HALF], F32, name="early1", tag="a0_bf", align_bytes=64),
         ]
-        on_vector = ((0, 0), (0, 1), (1, 0))
-        for t, d in on_vector:
-            gather(early[d][:, t, :], t, d, 0, HALF, nc.vector)
         for d in range(2):
-            for t in range(PACK):
-                if (t, d) not in on_vector:
-                    gather(early[d][:, t, :], t, d, 0, HALF, nc.scalar)
+            gather(early[d][:, 0, :], 0, d, 0, HALF, nc.vector)
+        gather(early[0][:, 1, 0:P], 1, 0, 0, P, nc.vector)
+        gather(early[0][:, 1, P:HALF], 1, 0, P, P, nc.scalar)
+        for d in range(2):
+            for t in range(2 - d, PACK):
+                gather(early[d][:, t, :], t, d, 0, HALF, nc.scalar)
 
         w3_src = w3_raw[:].rearrange("p j (q t r) -> p t q j r", t=PACK, r=RUN)
         w3_bf = [sb.tile([P, 2 * PASS], BF16, name="w3_bf%d" % b, align_bytes=64) for b in range(2)]

@@ -22,6 +22,7 @@ PACK = 4
 PASS = P * PACK
 RUN = 2
 HALF = T // 2
+THIRD = 128
 PER_COLUMN = 16
 
 
@@ -157,6 +158,20 @@ def tile_picked_wdime_silu_l_kernel(tc, x_words, x_scales, aT, w1, w3, w2, pos1,
                 )
             return bank
 
+        def filters_wide(codes, scales, tags):
+            banks = [ps.tile([P, 2, HALF], F32, name="f_wide", tag=tag) for tag in tags]
+            for t in range(PACK):
+                nc.tensor.matmul_mx(
+                    out=banks[t // 2][:, t % 2, :],
+                    lhsT=w3_q[t // 2][0][:, t % 2 * P : (t % 2 + 1) * P].bitcast(FP8X4),
+                    lhsT_scale=w3_q[t // 2][1][:, t % 2 * P : (t % 2 + 1) * P],
+                    rhs=codes[:].bitcast(FP8X4),
+                    rhs_scale=scales[:],
+                    start=True,
+                    stop=True,
+                )
+            return banks
+
         def multiply(product, picked, bank):
             nc.vector.tensor_tensor(
                 product.rearrange("p (c r t) -> p c t r", r=RUN, t=PACK),
@@ -165,24 +180,30 @@ def tile_picked_wdime_silu_l_kernel(tc, x_words, x_scales, aT, w1, w3, w2, pos1,
                 MULT,
             )
 
-        def project(name, codes, scales, v0, width, tags):
-            banks = {tag: ps.tile([P, tags.count(tag), width], F32, name=name + tag, tag=tag) for tag in sorted(set(tags))}
-            for m in range(N // P):
+        def add_woven(z, v0, v1):
+            nc.vector.tensor_tensor(
+                z.rearrange("p (c r t) -> p c t r", r=RUN, t=PACK),
+                plain[0][:, :, v0:v1].rearrange("p t (c r) -> p c t r", r=RUN),
+                plain[1][:, :, v0:v1].rearrange("p t (c r) -> p c t r", r=RUN),
+                ADD,
+            )
+
+        def project(name, z_q, v0, width, rows, tag):
+            bank = ps.tile([P, len(rows), width], F32, name=name + "_bank", tag=tag)
+            for s, m in enumerate(rows):
                 nc.tensor.matmul_mx(
-                    out=banks[tags[m]][:, m - tags.index(tags[m]), :],
-                    lhsT=w2_codes[:, m * P : (m + 1) * P].bitcast(FP8X4),
-                    lhsT_scale=w2_scales[:, m * P : (m + 1) * P],
-                    rhs=codes.bitcast(FP8X4),
-                    rhs_scale=scales,
+                    out=bank[:, s, :],
+                    lhsT=w2_q[m][0][:].bitcast(FP8X4),
+                    lhsT_scale=w2_q[m][1][:],
+                    rhs=z_q[0][:].bitcast(FP8X4),
+                    rhs_scale=z_q[1][:],
                     start=True,
                     stop=True,
                 )
-            rows = out.rearrange("(m p) v -> p m v", p=P)
-            for tag, bank in banks.items():
-                m0, m1 = tags.index(tag), tags.index(tag) + tags.count(tag)
-                result = sb.tile([P, m1 - m0, width], F32, name=name + tag + "_o")
-                nc.scalar.activation(result[:], bank[:], SILU)
-                nc.sync.dma_start(out=rows[:, m0:m1, v0 : v0 + width], in_=result[:])
+            result = sb.tile([P, len(rows), width], F32, name=name + "_o")
+            nc.scalar.activation(result[:], bank[:], SILU)
+            blocks = out.rearrange("(m p) v -> p m v", p=P)
+            nc.sync.dma_start(out=blocks[:, rows[0] : rows[-1] + 1, v0 : v0 + width], in_=result[:])
 
         a0_bf = sb.tile([P, HALF * PACK], BF16, name="a0_bf", align_bytes=64)
         for c in range(2):
@@ -198,8 +219,8 @@ def tile_picked_wdime_silu_l_kernel(tc, x_words, x_scales, aT, w1, w3, w2, pos1,
         ]
         for d in range(2):
             gather(early[d][:, 0, :], 0, d, 0, HALF, nc.vector)
-        gather(early[0][:, 1, 0:P], 1, 0, 0, P, nc.vector)
-        gather(early[0][:, 1, P:HALF], 1, 0, P, P, nc.scalar)
+        gather(early[0][:, 1, 0:THIRD], 1, 0, 0, THIRD, nc.vector)
+        gather(early[0][:, 1, THIRD:HALF], 1, 0, THIRD, HALF - THIRD, nc.scalar)
         for d in range(2):
             for t in range(2 - d, PACK):
                 gather(early[d][:, t, :], t, d, 0, HALF, nc.scalar)
@@ -213,11 +234,9 @@ def tile_picked_wdime_silu_l_kernel(tc, x_words, x_scales, aT, w1, w3, w2, pos1,
         late = [shared.tile([P, PACK, HALF], F32, name="late%d" % d, offset=8192 + 4096 * d, align_bytes=64) for d in range(2)]
         for t in range(PACK):
             gather(late[1][:, t, :], t, 1, HALF, HALF, nc.scalar)
-        for t in range(PACK - 1):
+        for t in range(PACK):
             gather(late[0][:, t, :], t, 0, HALF, HALF, nc.scalar)
-        for c in range(2):
-            gather(late[0][:, PACK - 1, c * P : (c + 1) * P], PACK - 1, 0, HALF + c * P, P, nc.scalar)
-        w2_bf = rounded("w2", w2_raw[:], N, nc.scalar.copy)
+        w2_bf = [rounded("w2_%d" % m, w2_raw[:, :, m * P : (m + 1) * P], P, nc.scalar.copy) for m in range(N // P)]
         w3_q = [quantise("w3_%d" % b, w3_bf[b][:], 2 * P) for b in range(2)]
         f0 = [filters(*a0, 0, "b4"), filters(*a0, P, "b5")]
         a1_bf = shared.tile([P, HALF * PACK], BF16, name="a1_bf", offset=16384 + 1024, align_bytes=64)
@@ -227,7 +246,7 @@ def tile_picked_wdime_silu_l_kernel(tc, x_words, x_scales, aT, w1, w3, w2, pos1,
         a1 = quantise("a1", a1_bf[:], HALF)
         f1 = [filters(*a1, 0, "b6"), filters(*a1, P, "b7")]
         a3 = quantise("a3", a3_bf[:], HALF)
-        f1 += [filters(*a3, 0, "b0"), filters(*a3, P, "b1")]
+        f1 += filters_wide(*a3, ("b0", "b1"))
         a2_bf = shared.tile([P, HALF * PACK], BF16, name="a2_bf", offset=24576, align_bytes=64)
         nc.gpsimd.tensor_scalar(
             a2_bf[:].rearrange("p (c j) -> p c j", j=PACK), a_last[:].rearrange("p j c -> p c j"), 1.0, 0.0, MULT, ADD
@@ -236,14 +255,10 @@ def tile_picked_wdime_silu_l_kernel(tc, x_words, x_scales, aT, w1, w3, w2, pos1,
         p0 = [
             shared.tile([P, PASS], F32, name="p0_0", offset=16384, align_bytes=64),
             shared.tile([P, PASS], F32, name="p0_1", offset=16384 + 2048, align_bytes=64),
-            sb.tile([P, PASS], F32, name="p0_2", align_bytes=64),
-            sb.tile([P, PASS], F32, name="p0_3", align_bytes=64),
         ]
         p1 = [
             sb.tile([P, PASS], F32, name="p1_0", align_bytes=64),
             sb.tile([P, PASS], F32, name="p1_1", align_bytes=64),
-            shared.tile([P, PASS], F32, name="p1_2", offset=24576 - 2048 + 64, align_bytes=64),
-            sb.tile([P, PASS], F32, name="p1_3", tag="a0_bf", align_bytes=64),
         ]
         multiply(p0[0][:], early[0][:, :, 0:P], f0[0])
         multiply(p0[1][:], early[0][:, :, P:HALF], f0[1])
@@ -251,23 +266,39 @@ def tile_picked_wdime_silu_l_kernel(tc, x_words, x_scales, aT, w1, w3, w2, pos1,
         a2_codes = shared.tile([P, HALF], U32, name="a2_codes", offset=0, align_bytes=64)
         a2_scales = sb.tile([P, HALF], U8, name="a2_scales", align_bytes=64)
         a2 = quantise_into(a2_codes[:], a2_scales[:], a2_bf[:])
-        f0 += [filters(*a2, 0, "b2"), filters(*a2, P, "b3")]
+        f0 += filters_wide(*a2, ("b2", "b3"))
         z_first = shared.tile([P, 2 * PASS], BF16, name="z_first", offset=24576 + 64, align_bytes=64)
         nc.gpsimd.tensor_tensor(z_first[:, 0:PASS], p0[0][:], p1[0][:], ADD)
         multiply(p1[1][:], early[1][:, :, P:HALF], f1[1])
         nc.gpsimd.tensor_tensor(z_first[:, PASS : 2 * PASS], p0[1][:], p1[1][:], ADD)
-        multiply(p1[2][:], late[1][:, :, 0:P], f1[2])
-        multiply(p1[3][:], late[1][:, :, P:HALF], f1[3])
-        multiply(p0[2][:], late[0][:, :, 0:P], f0[2])
-        multiply(p0[3][:], late[0][:, :, P:HALF], f0[3])
+        plain = [
+            sb.tile([P, PACK, HALF], F32, name="plain0", align_bytes=64),
+            shared.tile([P, PACK, HALF], F32, name="plain1", offset=24576 - 4096 + 64, align_bytes=64),
+        ]
+        for b in range(2):
+            nc.vector.tensor_tensor(plain[1][:, 2 * b : 2 * b + 2, :], late[1][:, 2 * b : 2 * b + 2, :], f1[2 + b][:], MULT)
+        nc.vector.tensor_tensor(plain[0][:, 0:2, :], late[0][:, 0:2, :], f0[2][:], MULT)
+        for t in range(2, PACK):
+            nc.vector.tensor_tensor(plain[0][:, t, :], late[0][:, t, :], f0[3][:, t - 2, :], MULT)
         zf = quantise("zf", z_first[:], HALF)
-        w2_codes, w2_scales = quantise("w2", w2_bf[:], N)
-        project("o0", zf[0][:], zf[1][:], 0, HALF, ("b4", "b5"))
-        z = [sb.tile([P, PASS], BF16, name="z%d" % c, tag=("w2_raw", "w2_bf")[c], align_bytes=64) for c in range(2)]
-        nc.vector.tensor_tensor(z[0][:], p0[2][:], p1[2][:], ADD)
-        nc.vector.tensor_tensor(z[1][:, 0:HALF], p0[3][:, 0:HALF], p1[3][:, 0:HALF], ADD)
-        codes, scales = quantise("z2", z[0][:], P)
-        project("o1", codes[:], scales[:], HALF, P, ("b6", "b6"))
-        nc.vector.tensor_tensor(z[1][:, HALF:PASS], p0[3][:, HALF:PASS], p1[3][:, HALF:PASS], ADD)
-        codes, scales = quantise("z3", z[1][:], P)
-        project("o2", codes[:], scales[:], HALF + P, P, ("b7", "b0"))
+        w2_q = [quantise("w2_0", w2_bf[0][:], P)]
+        project("o0_0", zf, 0, HALF, (0,), "b4")
+        z = [shared.tile([P, PASS], BF16, name="z0", offset=24576 + 64, align_bytes=64)]
+        add_woven(z[0][:], 0, P)
+        w2_q.append(quantise("w2_1", w2_bf[1][:], P))
+        project("o0_1", zf, 0, HALF, (1,), "b5")
+        z.append(sb.tile([P, PASS], BF16, name="z1", tag="w2_0_bf", align_bytes=64))
+        add_woven(z[1][:, 0:HALF], P, P + P // 2)
+        z2 = quantise("z2", z[0][:], P)
+        for m in range(N // P):
+            project("o1_%d" % m, z2, HALF, P, (m,), ("b6", "b1")[m])
+        add_woven(z[1][:, HALF:PASS], P + P // 2, HALF)
+        z3 = (
+            sb.tile([P, P], U32, name="z3_codes", align_bytes=64),
+            sb.tile([P, P], U8, name="z3_scales", align_bytes=64),
+        )
+        for u in range(2):
+            columns = slice(u * P // 2, (u + 1) * P // 2)
+            quantise_into(z3[0][:, columns], z3[1][:, columns], z[1][:, u * HALF : (u + 1) * HALF])
+        for m in range(N // P):
+            project("o2_%d" % m, z3, HALF + P, P, (m,), ("b7", "b0")[m])

@@ -243,18 +243,18 @@ def tile_picked_wdime_silu_l_kernel(tc, x_words, x_scales, aT, w1, w3, w2, pos1,
         round_into(a1_bf[:], a_list1[:, :, 0:HALF], nc.vector.tensor_copy)
         a3_bf = shared.tile([P, HALF * PACK], BF16, name="a3_bf", offset=24576, align_bytes=64)
         round_into(a3_bf[:], a_list1[:, :, HALF:T], nc.vector.tensor_copy)
-        a1 = quantise("a1", a1_bf[:], HALF)
+        a1 = quantise("a1", a1_bf[:], HALF, tag="a_codes")
         f1 = [filters(*a1, 0, "b6"), filters(*a1, P, "b7")]
         a3 = quantise("a3", a3_bf[:], HALF)
         f1 += filters_wide(*a3, ("b0", "b1"))
-        a2_bf = shared.tile([P, HALF * PACK], BF16, name="a2_bf", offset=24576, align_bytes=64)
+        a2_bf = shared.tile([P, HALF * PACK], BF16, name="a2_bf", offset=18432, align_bytes=64)
         nc.gpsimd.tensor_scalar(
             a2_bf[:].rearrange("p (c j) -> p c j", j=PACK), a_last[:].rearrange("p j c -> p c j"), 1.0, 0.0, MULT, ADD
         )
 
         p0 = [
             shared.tile([P, PASS], F32, name="p0_0", offset=16384, align_bytes=64),
-            shared.tile([P, PASS], F32, name="p0_1", offset=16384 + 2048, align_bytes=64),
+            shared.tile([P, PASS], F32, name="p0_1", offset=24576, align_bytes=64),
         ]
         p1 = [
             sb.tile([P, PASS], F32, name="p1_0", align_bytes=64),
@@ -263,17 +263,15 @@ def tile_picked_wdime_silu_l_kernel(tc, x_words, x_scales, aT, w1, w3, w2, pos1,
         multiply(p0[0][:], early[0][:, :, 0:P], f0[0])
         multiply(p0[1][:], early[0][:, :, P:HALF], f0[1])
         multiply(p1[0][:], early[1][:, :, 0:P], f1[0])
-        a2_codes = shared.tile([P, HALF], U32, name="a2_codes", offset=0, align_bytes=64)
-        a2_scales = sb.tile([P, HALF], U8, name="a2_scales", align_bytes=64)
-        a2 = quantise_into(a2_codes[:], a2_scales[:], a2_bf[:])
+        a2 = quantise("a2", a2_bf[:], HALF, tag="a_codes")
         f0 += filters_wide(*a2, ("b2", "b3"))
-        z_first = shared.tile([P, 2 * PASS], BF16, name="z_first", offset=24576 + 64, align_bytes=64)
+        z_first = shared.tile([P, 2 * PASS], BF16, name="z_first", offset=28672, align_bytes=64)
         nc.gpsimd.tensor_tensor(z_first[:, 0:PASS], p0[0][:], p1[0][:], ADD)
         multiply(p1[1][:], early[1][:, :, P:HALF], f1[1])
         nc.gpsimd.tensor_tensor(z_first[:, PASS : 2 * PASS], p0[1][:], p1[1][:], ADD)
         plain = [
             sb.tile([P, PACK, HALF], F32, name="plain0", align_bytes=64),
-            shared.tile([P, PACK, HALF], F32, name="plain1", offset=24576 - 4096 + 64, align_bytes=64),
+            shared.tile([P, PACK, HALF], F32, name="plain1", offset=20480 - 64, align_bytes=64),
         ]
         for b in range(2):
             nc.vector.tensor_tensor(plain[1][:, 2 * b : 2 * b + 2, :], late[1][:, 2 * b : 2 * b + 2, :], f1[2 + b][:], MULT)
@@ -283,7 +281,7 @@ def tile_picked_wdime_silu_l_kernel(tc, x_words, x_scales, aT, w1, w3, w2, pos1,
         zf = quantise("zf", z_first[:], HALF)
         w2_q = [quantise("w2_0", w2_bf[0][:], P)]
         project("o0_0", zf, 0, HALF, (0,), "b4")
-        z = [shared.tile([P, PASS], BF16, name="z0", offset=24576 + 64, align_bytes=64)]
+        z = [shared.tile([P, PASS], BF16, name="z0", offset=28672, align_bytes=64)]
         add_woven(z[0][:], 0, P)
         w2_q.append(quantise("w2_1", w2_bf[1][:], P))
         project("o0_1", zf, 0, HALF, (1,), "b5")

@@ -22,7 +22,8 @@ PACK = 4
 PASS = P * PACK
 RUN = 2
 HALF = T // 2
-THIRD = 128
+THIRD = 96
+CUT = 44
 PER_COLUMN = 16
 
 
@@ -100,14 +101,14 @@ def tile_picked_wdime_silu_l_kernel(tc, x_words, x_scales, aT, w1, w3, w2, pos1,
                 copy(out=grouped[t][:].rearrange("p (q r j) -> p q j r", r=RUN, j=PACK)[:, q0:q1], in_=src[:, t, q0:q1])
 
             pairs = P // RUN
-            round_plane(0, 0, pairs // 2, nc.vector.tensor_copy)
-            round_plane(0, pairs // 2, pairs, nc.scalar.copy)
+            round_plane(0, 0, CUT, nc.vector.tensor_copy)
+            round_plane(0, CUT, pairs, nc.scalar.copy)
             round_plane(1, 0, pairs, nc.scalar.copy)
             round_plane(2, 0, pairs, nc.vector.tensor_copy)
             planes = {t: quantise("w1_%d_%d" % (g, t), grouped[t][:], P) for t in (0, 2)}
             grouped.append(sb.tile([P, PASS], BF16, name="w1_%d_bf3" % g, tag="w1_%d_bf0" % g, align_bytes=64))
-            round_plane(3, 0, pairs // 2, nc.vector.tensor_copy)
-            round_plane(3, pairs // 2, pairs, nc.scalar.copy)
+            round_plane(3, 0, CUT, nc.vector.tensor_copy)
+            round_plane(3, CUT, pairs, nc.scalar.copy)
             for t in (1, 3):
                 planes[t] = quantise("w1_%d_%d" % (g, t), grouped[t][:], P)
             w1_q += [planes[t] for t in range(PACK)]
@@ -234,8 +235,10 @@ def tile_picked_wdime_silu_l_kernel(tc, x_words, x_scales, aT, w1, w3, w2, pos1,
         late = [shared.tile([P, PACK, HALF], F32, name="late%d" % d, offset=8192 + 4096 * d, align_bytes=64) for d in range(2)]
         for t in range(PACK):
             gather(late[1][:, t, :], t, 1, HALF, HALF, nc.scalar)
-        for t in range(PACK):
+        for t in range(PACK - 1):
             gather(late[0][:, t, :], t, 0, HALF, HALF, nc.scalar)
+        for c in range(2):
+            gather(late[0][:, PACK - 1, c * P : (c + 1) * P], PACK - 1, 0, HALF + c * P, P, nc.scalar)
         w2_bf = [rounded("w2_%d" % m, w2_raw[:, :, m * P : (m + 1) * P], P, nc.scalar.copy) for m in range(N // P)]
         w3_q = [quantise("w3_%d" % b, w3_bf[b][:], 2 * P) for b in range(2)]
         f0 = [filters(*a0, 0, "b4"), filters(*a0, P, "b5")]
@@ -265,7 +268,8 @@ def tile_picked_wdime_silu_l_kernel(tc, x_words, x_scales, aT, w1, w3, w2, pos1,
         multiply(p1[0][:], early[1][:, :, 0:P], f1[0])
         a2 = quantise("a2", a2_bf[:], HALF, tag="a_codes")
         f0 += filters_wide(*a2, ("b2", "b3"))
-        z_first = shared.tile([P, 2 * PASS], BF16, name="z_first", offset=28672, align_bytes=64)
+        sums = sb.tile([P, HALF + 2 * PASS], BF16, name="sums", align_bytes=64)
+        z_first, z = sums[:, HALF:], [sums[:, 0:PASS]]
         nc.gpsimd.tensor_tensor(z_first[:, 0:PASS], p0[0][:], p1[0][:], ADD)
         multiply(p1[1][:], early[1][:, :, P:HALF], f1[1])
         nc.gpsimd.tensor_tensor(z_first[:, PASS : 2 * PASS], p0[1][:], p1[1][:], ADD)
@@ -276,18 +280,20 @@ def tile_picked_wdime_silu_l_kernel(tc, x_words, x_scales, aT, w1, w3, w2, pos1,
         for b in range(2):
             nc.vector.tensor_tensor(plain[1][:, 2 * b : 2 * b + 2, :], late[1][:, 2 * b : 2 * b + 2, :], f1[2 + b][:], MULT)
         nc.vector.tensor_tensor(plain[0][:, 0:2, :], late[0][:, 0:2, :], f0[2][:], MULT)
-        for t in range(2, PACK):
-            nc.vector.tensor_tensor(plain[0][:, t, :], late[0][:, t, :], f0[3][:, t - 2, :], MULT)
-        zf = quantise("zf", z_first[:], HALF)
+        nc.vector.tensor_tensor(plain[0][:, 2, :], late[0][:, 2, :], f0[3][:, 0, :], MULT)
+        for c in range(2):
+            block = slice(c * P, (c + 1) * P)
+            nc.vector.tensor_tensor(plain[0][:, 3, block], late[0][:, 3, block], f0[3][:, 1, block], MULT)
+        add_woven(z[0][:, 0:HALF], 0, P // 2)
+        zf = quantise("zf", z_first, HALF)
         w2_q = [quantise("w2_0", w2_bf[0][:], P)]
         project("o0_0", zf, 0, HALF, (0,), "b4")
-        z = [shared.tile([P, PASS], BF16, name="z0", offset=28672, align_bytes=64)]
-        add_woven(z[0][:], 0, P)
+        add_woven(z[0][:, HALF:PASS], P // 2, P)
         w2_q.append(quantise("w2_1", w2_bf[1][:], P))
         project("o0_1", zf, 0, HALF, (1,), "b5")
         z.append(sb.tile([P, PASS], BF16, name="z1", tag="w2_0_bf", align_bytes=64))
         add_woven(z[1][:, 0:HALF], P, P + P // 2)
-        z2 = quantise("z2", z[0][:], P)
+        z2 = quantise("z2", z[0], P)
         for m in range(N // P):
             project("o1_%d" % m, z2, HALF, P, (m,), ("b6", "b1")[m])
         add_woven(z[1][:, HALF:PASS], P + P // 2, HALF)

@@ -63,25 +63,25 @@ def tile_picked_wdime_silu_l_kernel(tc, x_words, x_scales, aT, w1, w3, w2, pos1,
         warm_out = sb.tile([P, 1], F32, name="warm2")
         nc.scalar.activation(warm_out[:], warm_in[:], SILU)
 
-        x_planes = sb.tile([P, T], U8, name="xs", align_bytes=64)
+        x_planes = sb.tile([P, 2 * T], U8, name="xs", align_bytes=64)
         nc.gpsimd.memset(x_planes[:].bitcast(I32), 0)
 
         w1_raw = [load_rows("w1_0", w1[0:PASS, :])]
-        for q in range(4):
+        for r in range(4):
             nc.sync.dma_start(
-                out=x_planes[32 * q : 32 * q + 8, :].bitcast(I32),
-                in_=x_scales[:, 4 * q : 4 * q + 4, :].bitcast(I32),
+                out=x_planes[r:P:32, :].bitcast(I32).rearrange("q (g c) -> q g c", g=2),
+                in_=x_scales.bitcast(I32)[:, r:16:4, :].rearrange("g q c -> q g c"),
             )
         x_codes = [load_words(0)]
         w1_raw.append(load_rows("w1_1", w1[PASS : 2 * PASS, :]))
         x_codes.append(load_words(1))
+        a_first = shared.tile([P, PACK, HALF], F32, name="a_first", offset=0, align_bytes=64)
+        nc.sync.dma_start(out=a_first[:], in_=aT[:, 0:HALF].rearrange("(p j) c -> p j c", j=PACK))
         lists = []
         for d, pos in enumerate((pos1, pos2)):
             offsets = sb.tile([P, T // PER_COLUMN], U16, name="offsets%d" % d)
             nc.sync.dma_start(offsets[:], pos)
             lists.append(offsets)
-        a_first = shared.tile([P, PACK, HALF], F32, name="a_first", offset=0, align_bytes=64)
-        nc.sync.dma_start(out=a_first[:], in_=aT[:, 0:HALF].rearrange("(p j) c -> p j c", j=PACK))
         w3_raw = shared.tile([P, PACK, H], F32, name="w3_raw", offset=8192, align_bytes=64)
         nc.sync.dma_start(out=w3_raw[:], in_=w3.rearrange("(p j) c -> p j c", j=PACK))
         a_list1 = load_rows("a_list1", aT[:, T : 2 * T])
@@ -92,6 +92,9 @@ def tile_picked_wdime_silu_l_kernel(tc, x_words, x_scales, aT, w1, w3, w2, pos1,
             nc.sync.dma_start(out=w2_raw[:, t, :], in_=w2_rows[t])
 
         h_banks = [ps.tile([P, T], F32, name="h_bank%d" % t, tag="b%d" % t) for t in range(PACK)]
+        h_second = ps.tile([P, HALF], F32, name="h_second", tag="b4")
+        h_parts = [(0, h_banks[0][:, 0:HALF], 0, HALF), (0, h_second[:], HALF, T)]
+        h_parts += [(t, h_banks[t][:], 0, T) for t in range(1, PACK)]
         w1_q = []
         for g in range(2):
             src = w1_raw[g][:].rearrange("p j (q t r) -> p t q j r", t=PACK, r=RUN)
@@ -114,19 +117,19 @@ def tile_picked_wdime_silu_l_kernel(tc, x_words, x_scales, aT, w1, w3, w2, pos1,
             w1_q += [planes[t] for t in range(PACK)]
         h = [sb.tile([P, T], F32, name="h%d" % t, align_bytes=64) for t in range(PACK)]
         for g in range(2):
-            for t in range(PACK):
+            for t, bank, c0, c1 in h_parts:
                 codes, scales = w1_q[PACK * g + t]
                 nc.tensor.matmul_mx(
-                    out=h_banks[t][:],
+                    out=bank,
                     lhsT=codes[:].bitcast(FP8X4),
                     lhsT_scale=scales[:],
-                    rhs=x_codes[g][:].bitcast(FP8X4),
-                    rhs_scale=x_planes[4 * g : P, :],
+                    rhs=x_codes[g][:, c0:c1].bitcast(FP8X4),
+                    rhs_scale=x_planes[:, g * T + c0 : g * T + c1],
                     start=(g == 0),
                     stop=(g == 1),
                 )
-        for t in range(PACK):
-            nc.scalar.activation(h[t][:], h_banks[t][:], SILU)
+        for t, bank, c0, c1 in h_parts:
+            nc.scalar.activation(h[t][:, c0:c1], bank, SILU)
 
         def gather(picked, t, d, v0, width, engine):
             window = h[t][:].indirect(lists[d][:, v0 // PER_COLUMN : (v0 + width) // PER_COLUMN])
@@ -189,7 +192,7 @@ def tile_picked_wdime_silu_l_kernel(tc, x_words, x_scales, aT, w1, w3, w2, pos1,
                 ADD,
             )
 
-        def project(name, z_q, v0, width, rows, tag):
+        def project(name, z_q, v0, width, rows, tag, queue=nc.sync):
             bank = ps.tile([P, len(rows), width], F32, name=name + "_bank", tag=tag)
             for s, m in enumerate(rows):
                 nc.tensor.matmul_mx(
@@ -204,7 +207,7 @@ def tile_picked_wdime_silu_l_kernel(tc, x_words, x_scales, aT, w1, w3, w2, pos1,
             result = sb.tile([P, len(rows), width], F32, name=name + "_o")
             nc.scalar.activation(result[:], bank[:], SILU)
             blocks = out.rearrange("(m p) v -> p m v", p=P)
-            nc.sync.dma_start(out=blocks[:, rows[0] : rows[-1] + 1, v0 : v0 + width], in_=result[:])
+            queue.dma_start(out=blocks[:, rows[0] : rows[-1] + 1, v0 : v0 + width], in_=result[:])
 
         a0_bf = sb.tile([P, HALF * PACK], BF16, name="a0_bf", align_bytes=64)
         for c in range(2):
@@ -305,4 +308,4 @@ def tile_picked_wdime_silu_l_kernel(tc, x_words, x_scales, aT, w1, w3, w2, pos1,
             columns = slice(u * P // 2, (u + 1) * P // 2)
             quantise_into(z3[0][:, columns], z3[1][:, columns], z[1][:, u * HALF : (u + 1) * HALF])
         for m in range(N // P):
-            project("o2_%d" % m, z3, HALF + P, P, (m,), ("b7", "b0")[m])
+            project("o2_%d" % m, z3, HALF + P, P, (m,), ("b7", "b0")[m], (nc.sync, nc.scalar)[m])

@@ -192,7 +192,7 @@ def tile_picked_wdime_silu_l_kernel(tc, x_words, x_scales, aT, w1, w3, w2, pos1,
                 ADD,
             )
 
-        def project(name, z_q, v0, width, rows, tag, queue=nc.sync):
+        def project(name, z_q, v0, width, rows, tag):
             bank = ps.tile([P, len(rows), width], F32, name=name + "_bank", tag=tag)
             for s, m in enumerate(rows):
                 nc.tensor.matmul_mx(
@@ -207,7 +207,7 @@ def tile_picked_wdime_silu_l_kernel(tc, x_words, x_scales, aT, w1, w3, w2, pos1,
             result = sb.tile([P, len(rows), width], F32, name=name + "_o")
             nc.scalar.activation(result[:], bank[:], SILU)
             blocks = out.rearrange("(m p) v -> p m v", p=P)
-            queue.dma_start(out=blocks[:, rows[0] : rows[-1] + 1, v0 : v0 + width], in_=result[:])
+            nc.sync.dma_start(out=blocks[:, rows[0] : rows[-1] + 1, v0 : v0 + width], in_=result[:])
 
         a0_bf = sb.tile([P, HALF * PACK], BF16, name="a0_bf", align_bytes=64)
         for c in range(2):
@@ -308,4 +308,4 @@ def tile_picked_wdime_silu_l_kernel(tc, x_words, x_scales, aT, w1, w3, w2, pos1,
             columns = slice(u * P // 2, (u + 1) * P // 2)
             quantise_into(z3[0][:, columns], z3[1][:, columns], z[1][:, u * HALF : (u + 1) * HALF])
         for m in range(N // P):
-            project("o2_%d" % m, z3, HALF + P, P, (m,), ("b7", "b0")[m], (nc.sync, nc.scalar)[m])
+            project("o2_%d" % m, z3, HALF + P, P, (m,), ("b7", "b0")[m])

@@ -24,6 +24,7 @@ RUN = 2
 HALF = T // 2
 THIRD = 96
 CUT = 44
+WHOLE = 2
 PER_COLUMN = 16
 
 
@@ -115,7 +116,9 @@ def tile_picked_wdime_silu_l_kernel(tc, x_words, x_scales, aT, w1, w3, w2, pos1,
             for t in (1, 3):
                 planes[t] = quantise("w1_%d_%d" % (g, t), grouped[t][:], P)
             w1_q += [planes[t] for t in range(PACK)]
-        h = [sb.tile([P, T], F32, name="h%d" % t, align_bytes=64) for t in range(PACK)]
+        h = [sb.tile([P, T + PER_COLUMN * (t >= WHOLE)], F32, name="h%d" % t, align_bytes=64) for t in range(PACK)]
+        for t in range(WHOLE, PACK):
+            nc.vector.memset(h[t][:, T:], 0.0)
         for g in range(2):
             for t, bank, c0, c1 in h_parts:
                 codes, scales = w1_q[PACK * g + t]
@@ -219,15 +222,16 @@ def tile_picked_wdime_silu_l_kernel(tc, x_words, x_scales, aT, w1, w3, w2, pos1,
         a0 = a0_codes, a0_scales
         early = [
             shared.tile([P, PACK, HALF], F32, name="early0", offset=0, align_bytes=64),
-            sb.tile([P, PACK, HALF], F32, name="early1", tag="a0_bf", align_bytes=64),
+            sb.tile([P, PACK, T], F32, name="early1", tag="a0_bf", align_bytes=64),
         ]
         for d in range(2):
-            gather(early[d][:, 0, :], 0, d, 0, HALF, nc.vector)
+            gather(early[d][:, 0, 0:HALF], 0, d, 0, HALF, nc.vector)
         gather(early[0][:, 1, 0:THIRD], 1, 0, 0, THIRD, nc.vector)
         gather(early[0][:, 1, THIRD:HALF], 1, 0, THIRD, HALF - THIRD, nc.scalar)
         for d in range(2):
             for t in range(2 - d, PACK):
-                gather(early[d][:, t, :], t, d, 0, HALF, nc.scalar)
+                width = T if d == 1 and t >= WHOLE else HALF
+                gather(early[d][:, t, 0:width], t, d, 0, width, nc.scalar)
 
         w3_src = w3_raw[:].rearrange("p j (q t r) -> p t q j r", t=PACK, r=RUN)
         w3_bf = [sb.tile([P, 2 * PASS], BF16, name="w3_bf%d" % b, align_bytes=64) for b in range(2)]
@@ -236,7 +240,7 @@ def tile_picked_wdime_silu_l_kernel(tc, x_words, x_scales, aT, w1, w3, w2, pos1,
                 out=w3_bf[b][:].rearrange("p (t q r j) -> p t q j r", t=2, r=RUN, j=PACK), in_=w3_src[:, 2 * b : 2 * b + 2]
             )
         late = [shared.tile([P, PACK, HALF], F32, name="late%d" % d, offset=8192 + 4096 * d, align_bytes=64) for d in range(2)]
-        for t in range(PACK):
+        for t in range(WHOLE):
             gather(late[1][:, t, :], t, 1, HALF, HALF, nc.scalar)
         for t in range(PACK - 1):
             gather(late[0][:, t, :], t, 0, HALF, HALF, nc.scalar)
@@ -280,8 +284,8 @@ def tile_picked_wdime_silu_l_kernel(tc, x_words, x_scales, aT, w1, w3, w2, pos1,
             sb.tile([P, PACK, HALF], F32, name="plain0", align_bytes=64),
             shared.tile([P, PACK, HALF], F32, name="plain1", offset=20480 - 64, align_bytes=64),
         ]
-        for b in range(2):
-            nc.vector.tensor_tensor(plain[1][:, 2 * b : 2 * b + 2, :], late[1][:, 2 * b : 2 * b + 2, :], f1[2 + b][:], MULT)
+        nc.vector.tensor_tensor(plain[1][:, 0:2, :], late[1][:, 0:2, :], f1[2][:], MULT)
+        nc.vector.tensor_tensor(plain[1][:, 2:4, :], early[1][:, 2:4, HALF:T], f1[3][:], MULT)
         nc.vector.tensor_tensor(plain[0][:, 0:2, :], late[0][:, 0:2, :], f0[2][:], MULT)
         nc.vector.tensor_tensor(plain[0][:, 2, :], late[0][:, 2, :], f0[3][:, 0, :], MULT)
         for c in range(2):

@@ -22,7 +22,6 @@ PACK = 4
 PASS = P * PACK
 RUN = 2
 HALF = T // 2
-THIRD = 96
 CUT = 44
 WHOLE = 2
 PER_COLUMN = 16
@@ -226,10 +225,8 @@ def tile_picked_wdime_silu_l_kernel(tc, x_words, x_scales, aT, w1, w3, w2, pos1,
         ]
         for d in range(2):
             gather(early[d][:, 0, 0:HALF], 0, d, 0, HALF, nc.vector)
-        gather(early[0][:, 1, 0:THIRD], 1, 0, 0, THIRD, nc.vector)
-        gather(early[0][:, 1, THIRD:HALF], 1, 0, THIRD, HALF - THIRD, nc.scalar)
         for d in range(2):
-            for t in range(2 - d, PACK):
+            for t in range(1, PACK):
                 width = T if d == 1 and t >= WHOLE else HALF
                 gather(early[d][:, t, 0:width], t, d, 0, width, nc.scalar)
 

@@ -66,6 +66,10 @@ def tile_picked_wdime_silu_l_kernel(tc, x_words, x_scales, aT, w1, w3, w2, pos1,
         x_planes = sb.tile([P, 2 * T], U8, name="xs", align_bytes=64)
         nc.gpsimd.memset(x_planes[:].bitcast(I32), 0)
 
+        warm_pool = sb.tile([P, 2], BF16, name="warm_pool")
+        nc.gpsimd.tensor_scalar(warm_pool[:, 0:1], warm_in[:], 1.0, 0.0, MULT, ADD)
+        nc.gpsimd.tensor_tensor(warm_pool[:, 1:2], warm_in[:], warm_in[:], ADD)
+
         w1_raw = [load_rows("w1_0", w1[0:PASS, :])]
         for r in range(4):
             nc.sync.dma_start(

from contextlib import ExitStack

import concourse.mybir as mybir

K, T, H, N, J, U = 1024, 512, 512, 256, 512, 1024
FLOPS = 2 * (K * H * T + J * H * U + H * N * T)

F32 = mybir.dt.float32
BF16 = mybir.dt.bfloat16
I32 = mybir.dt.int32
U32 = mybir.dt.uint32
U16 = mybir.dt.uint16
U8 = mybir.dt.uint8
FP8X4 = mybir.dt.float8_e4m3fn_x4
COPY = mybir.ActivationFunctionType.Copy
SILU = mybir.ActivationFunctionType.Silu
MULT = mybir.AluOpType.mult
ADD = mybir.AluOpType.add

P = 128
PACK = 4
PASS = P * PACK
RUN = 2
HALF = T // 2
CUT = 44
WHOLE = 2
PER_COLUMN = 16


def tile_picked_wdime_silu_l_kernel(tc, x_words, x_scales, aT, w1, w3, w2, pos1, pos2, out):
    nc = tc.nc
    with ExitStack() as ctx:
        sb = ctx.enter_context(tc.tile_pool(name="sb", bufs=1))
        shared = ctx.enter_context(tc.tile_pool(name="shared", bufs=1))
        ps = ctx.enter_context(tc.psum_pool(name="ps", bufs=1))

        def quantise(name, grouped, width, tag=None):
            codes = sb.tile([P, width], U32, name=name + "_codes", tag=tag or name + "_codes", align_bytes=64)
            scales = sb.tile([P, width], U8, name=name + "_scales", align_bytes=64)
            nc.vector.quantize_mx(out=codes[:].bitcast(FP8X4), scales=scales[:], in_=grouped)
            return codes, scales

        def load_rows(name, rows):
            raw = sb.tile([P, PACK, rows.shape[1]], F32, name=name + "_raw", align_bytes=64)
            nc.sync.dma_start(out=raw[:], in_=rows.rearrange("(p j) c -> p j c", j=PACK))
            return raw

        def load_words(g):
            words = sb.tile([P, T], U32, name="xw%d" % g, align_bytes=64)
            nc.sync.dma_start(out=words[:].bitcast(I32), in_=x_words[g].rearrange("p c r -> p (c r)").bitcast(I32))
            return words

        def rounded(name, raw, width, copy, tag=None):
            grouped = sb.tile([P, width * PACK], BF16, name=name + "_bf", tag=tag or name + "_bf", align_bytes=64)
            copy(
                out=grouped[:].rearrange("p (c r j) -> p c j r", r=RUN, j=PACK),
                in_=raw.rearrange("p j (c r) -> p c j r", r=RUN),
            )
            return grouped

        warm_in = sb.tile([P, 1], F32, name="warm")
        nc.vector.memset(warm_in[:], 0.0)
        warm_out = sb.tile([P, 1], F32, name="warm2")
        nc.scalar.activation(warm_out[:], warm_in[:], SILU)

        x_planes = sb.tile([P, 2 * T], U8, name="xs", align_bytes=64)
        nc.gpsimd.memset(x_planes[:].bitcast(I32), 0)

        warm_pool = sb.tile([P, 2], BF16, name="warm_pool")
        nc.gpsimd.tensor_scalar(warm_pool[:, 0:1], warm_in[:], 1.0, 0.0, MULT, ADD)
        nc.gpsimd.tensor_tensor(warm_pool[:, 1:2], warm_in[:], warm_in[:], ADD)

        w1_raw = [load_rows("w1_0", w1[0:PASS, :])]
        for r in range(4):
            nc.sync.dma_start(
                out=x_planes[r:P:32, :].bitcast(I32).rearrange("q (g c) -> q g c", g=2),
                in_=x_scales.bitcast(I32)[:, r:16:4, :].rearrange("g q c -> q g c"),
            )
        x_codes = [load_words(0)]
        w1_raw.append(load_rows("w1_1", w1[PASS : 2 * PASS, :]))
        x_codes.append(load_words(1))
        a_first = shared.tile([P, PACK, HALF], F32, name="a_first", offset=0, align_bytes=64)
        nc.sync.dma_start(out=a_first[:], in_=aT[:, 0:HALF].rearrange("(p j) c -> p j c", j=PACK))
        lists = []
        for d, pos in enumerate((pos1, pos2)):
            offsets = sb.tile([P, T // PER_COLUMN], U16, name="offsets%d" % d)
            nc.sync.dma_start(offsets[:], pos)
            lists.append(offsets)
        w3_raw = shared.tile([P, PACK, H], F32, name="w3_raw", offset=8192, align_bytes=64)
        nc.sync.dma_start(out=w3_raw[:], in_=w3.rearrange("(p j) c -> p j c", j=PACK))
        a_list1 = load_rows("a_list1", aT[:, T : 2 * T])
        a_last = load_rows("a_last", aT[:, HALF:T])
        w2_raw = sb.tile([P, PACK, N], F32, name="w2_raw", align_bytes=64)
        w2_rows = w2.rearrange("(q t r) n -> t q r n", t=PACK, r=RUN)
        for t in range(PACK):
            nc.sync.dma_start(out=w2_raw[:, t, :], in_=w2_rows[t])

        h_banks = [ps.tile([P, T], F32, name="h_bank%d" % t, tag="b%d" % t) for t in range(PACK)]
        h_second = ps.tile([P, HALF], F32, name="h_second", tag="b4")
        h_parts = [(0, h_banks[0][:, 0:HALF], 0, HALF), (0, h_second[:], HALF, T)]
        h_parts += [(t, h_banks[t][:], 0, T) for t in range(1, PACK)]
        w1_q = []
        for g in range(2):
            src = w1_raw[g][:].rearrange("p j (q t r) -> p t q j r", t=PACK, r=RUN)
            grouped = [sb.tile([P, PASS], BF16, name="w1_%d_bf%d" % (g, t), align_bytes=64) for t in range(PACK - 1)]

            def round_plane(t, q0, q1, copy):
                copy(out=grouped[t][:].rearrange("p (q r j) -> p q j r", r=RUN, j=PACK)[:, q0:q1], in_=src[:, t, q0:q1])

            pairs = P // RUN
            round_plane(0, 0, CUT, nc.vector.tensor_copy)
            round_plane(0, CUT, pairs, nc.scalar.copy)
            round_plane(1, 0, pairs, nc.scalar.copy)
            round_plane(2, 0, pairs, nc.vector.tensor_copy)
            planes = {t: quantise("w1_%d_%d" % (g, t), grouped[t][:], P) for t in (0, 2)}
            grouped.append(sb.tile([P, PASS], BF16, name="w1_%d_bf3" % g, tag="w1_%d_bf0" % g, align_bytes=64))
            round_plane(3, 0, CUT, nc.vector.tensor_copy)
            round_plane(3, CUT, pairs, nc.scalar.copy)
            for t in (1, 3):
                planes[t] = quantise("w1_%d_%d" % (g, t), grouped[t][:], P)
            w1_q += [planes[t] for t in range(PACK)]
        h = [sb.tile([P, T + PER_COLUMN * (t >= WHOLE)], F32, name="h%d" % t, align_bytes=64) for t in range(PACK)]
        for t in range(WHOLE, PACK):
            nc.vector.memset(h[t][:, T:], 0.0)
        for g in range(2):
            for t, bank, c0, c1 in h_parts:
                codes, scales = w1_q[PACK * g + t]
                nc.tensor.matmul_mx(
                    out=bank,
                    lhsT=codes[:].bitcast(FP8X4),
                    lhsT_scale=scales[:],
                    rhs=x_codes[g][:, c0:c1].bitcast(FP8X4),
                    rhs_scale=x_planes[:, g * T + c0 : g * T + c1],
                    start=(g == 0),
                    stop=(g == 1),
                )
        for t, bank, c0, c1 in h_parts:
            nc.scalar.activation(h[t][:, c0:c1], bank, SILU)

        def gather(picked, t, d, v0, width, engine):
            window = h[t][:].indirect(lists[d][:, v0 // PER_COLUMN : (v0 + width) // PER_COLUMN])
            if engine is nc.vector:
                nc.vector.tensor_copy(picked, window)
            else:
                nc.scalar.activation(picked, window, COPY)

        def round_into(grouped, raw, copy):
            copy(
                out=grouped.rearrange("p (c r j) -> p c j r", r=RUN, j=PACK),
                in_=raw.rearrange("p j (c r) -> p c j r", r=RUN),
            )

        def quantise_into(codes, scales, grouped):
            nc.vector.quantize_mx(out=codes.bitcast(FP8X4), scales=scales, in_=grouped)
            return codes, scales

        def filters(codes, scales, c0, tag):
            bank = ps.tile([P, PACK, P], F32, name="f_bank", tag=tag)
            for t in range(PACK):
                nc.tensor.matmul_mx(
                    out=bank[:, t, :],
                    lhsT=w3_q[t // 2][0][:, t % 2 * P : (t % 2 + 1) * P].bitcast(FP8X4),
                    lhsT_scale=w3_q[t // 2][1][:, t % 2 * P : (t % 2 + 1) * P],
                    rhs=codes[:, c0 : c0 + P].bitcast(FP8X4),
                    rhs_scale=scales[:, c0 : c0 + P],
                    start=True,
                    stop=True,
                )
            return bank

        def filters_wide(codes, scales, tags):
            banks = [ps.tile([P, 2, HALF], F32, name="f_wide", tag=tag) for tag in tags]
            for t in range(PACK):
                nc.tensor.matmul_mx(
                    out=banks[t // 2][:, t % 2, :],
                    lhsT=w3_q[t // 2][0][:, t % 2 * P : (t % 2 + 1) * P].bitcast(FP8X4),
                    lhsT_scale=w3_q[t // 2][1][:, t % 2 * P : (t % 2 + 1) * P],
                    rhs=codes[:].bitcast(FP8X4),
                    rhs_scale=scales[:],
                    start=True,
                    stop=True,
                )
            return banks

        def multiply(product, picked, bank):
            nc.vector.tensor_tensor(
                product.rearrange("p (c r t) -> p c t r", r=RUN, t=PACK),
                picked.rearrange("p t (c r) -> p c t r", r=RUN),
                bank[:].rearrange("p t (c r) -> p c t r", r=RUN),
                MULT,
            )

        def add_woven(z, v0, v1):
            nc.vector.tensor_tensor(
                z.rearrange("p (c r t) -> p c t r", r=RUN, t=PACK),
                plain[0][:, :, v0:v1].rearrange("p t (c r) -> p c t r", r=RUN),
                plain[1][:, :, v0:v1].rearrange("p t (c r) -> p c t r", r=RUN),
                ADD,
            )

        def project(name, z_q, v0, width, rows, tag):
            bank = ps.tile([P, len(rows), width], F32, name=name + "_bank", tag=tag)
            for s, m in enumerate(rows):
                nc.tensor.matmul_mx(
                    out=bank[:, s, :],
                    lhsT=w2_q[m][0][:].bitcast(FP8X4),
                    lhsT_scale=w2_q[m][1][:],
                    rhs=z_q[0][:].bitcast(FP8X4),
                    rhs_scale=z_q[1][:],
                    start=True,
                    stop=True,
                )
            result = sb.tile([P, len(rows), width], F32, name=name + "_o")
            nc.scalar.activation(result[:], bank[:], SILU)
            blocks = out.rearrange("(m p) v -> p m v", p=P)
            nc.sync.dma_start(out=blocks[:, rows[0] : rows[-1] + 1, v0 : v0 + width], in_=result[:])

        a0_bf = sb.tile([P, HALF * PACK], BF16, name="a0_bf", align_bytes=64)
        for c in range(2):
            round_into(a0_bf[:, c * PASS : (c + 1) * PASS], a_first[:, :, c * P : (c + 1) * P], nc.vector.tensor_copy)
        a0_codes = sb.tile([P, HALF], U32, name="a0_codes", align_bytes=64)
        a0_scales = sb.tile([P, HALF], U8, name="a0_scales", align_bytes=64)
        for c in range(2):
            quantise_into(a0_codes[:, c * P : (c + 1) * P], a0_scales[:, c * P : (c + 1) * P], a0_bf[:, c * PASS : (c + 1) * PASS])
        a0 = a0_codes, a0_scales
        early = [
            shared.tile([P, PACK, HALF], F32, name="early0", offset=0, align_bytes=64),
            sb.tile([P, PACK, T], F32, name="early1", tag="a0_bf", align_bytes=64),
        ]
        for d in range(2):
            gather(early[d][:, 0, 0:HALF], 0, d, 0, HALF, nc.vector)
        for d in range(2):
            for t in range(1, PACK):
                width = T if d == 1 and t >= WHOLE else HALF
                gather(early[d][:, t, 0:width], t, d, 0, width, nc.scalar)

        w3_src = w3_raw[:].rearrange("p j (q t r) -> p t q j r", t=PACK, r=RUN)
        w3_bf = [sb.tile([P, 2 * PASS], BF16, name="w3_bf%d" % b, align_bytes=64) for b in range(2)]
        for b in range(2):
            nc.vector.tensor_copy(
                out=w3_bf[b][:].rearrange("p (t q r j) -> p t q j r", t=2, r=RUN, j=PACK), in_=w3_src[:, 2 * b : 2 * b + 2]
            )
        late = [shared.tile([P, PACK, HALF], F32, name="late%d" % d, offset=8192 + 4096 * d, align_bytes=64) for d in range(2)]
        for t in range(WHOLE):
            gather(late[1][:, t, :], t, 1, HALF, HALF, nc.scalar)
        for t in range(PACK - 1):
            gather(late[0][:, t, :], t, 0, HALF, HALF, nc.scalar)
        for c in range(2):
            gather(late[0][:, PACK - 1, c * P : (c + 1) * P], PACK - 1, 0, HALF + c * P, P, nc.scalar)
        w2_bf = [rounded("w2_%d" % m, w2_raw[:, :, m * P : (m + 1) * P], P, nc.scalar.copy) for m in range(N // P)]
        w3_q = [quantise("w3_%d" % b, w3_bf[b][:], 2 * P) for b in range(2)]
        f0 = [filters(*a0, 0, "b4"), filters(*a0, P, "b5")]
        a1_bf = shared.tile([P, HALF * PACK], BF16, name="a1_bf", offset=16384 + 1024, align_bytes=64)
        round_into(a1_bf[:], a_list1[:, :, 0:HALF], nc.vector.tensor_copy)
        a3_bf = shared.tile([P, HALF * PACK], BF16, name="a3_bf", offset=24576, align_bytes=64)
        round_into(a3_bf[:], a_list1[:, :, HALF:T], nc.vector.tensor_copy)
        a1 = quantise("a1", a1_bf[:], HALF, tag="a_codes")
        f1 = [filters(*a1, 0, "b6"), filters(*a1, P, "b7")]
        a3 = quantise("a3", a3_bf[:], HALF)
        f1 += filters_wide(*a3, ("b0", "b1"))
        a2_bf = shared.tile([P, HALF * PACK], BF16, name="a2_bf", offset=18432, align_bytes=64)
        nc.gpsimd.tensor_scalar(
            a2_bf[:].rearrange("p (c j) -> p c j", j=PACK), a_last[:].rearrange("p j c -> p c j"), 1.0, 0.0, MULT, ADD
        )

        p0 = [
            shared.tile([P, PASS], F32, name="p0_0", offset=16384, align_bytes=64),
            shared.tile([P, PASS], F32, name="p0_1", offset=24576, align_bytes=64),
        ]
        p1 = [
            sb.tile([P, PASS], F32, name="p1_0", align_bytes=64),
            sb.tile([P, PASS], F32, name="p1_1", align_bytes=64),
        ]
        multiply(p0[0][:], early[0][:, :, 0:P], f0[0])
        multiply(p0[1][:], early[0][:, :, P:HALF], f0[1])
        multiply(p1[0][:], early[1][:, :, 0:P], f1[0])
        a2 = quantise("a2", a2_bf[:], HALF, tag="a_codes")
        f0 += filters_wide(*a2, ("b2", "b3"))
        sums = sb.tile([P, HALF + 2 * PASS], BF16, name="sums", align_bytes=64)
        z_first, z = sums[:, HALF:], [sums[:, 0:PASS]]
        nc.gpsimd.tensor_tensor(z_first[:, 0:PASS], p0[0][:], p1[0][:], ADD)
        multiply(p1[1][:], early[1][:, :, P:HALF], f1[1])
        nc.gpsimd.tensor_tensor(z_first[:, PASS : 2 * PASS], p0[1][:], p1[1][:], ADD)
        plain = [
            sb.tile([P, PACK, HALF], F32, name="plain0", align_bytes=64),
            shared.tile([P, PACK, HALF], F32, name="plain1", offset=20480 - 64, align_bytes=64),
        ]
        nc.vector.tensor_tensor(plain[1][:, 0:2, :], late[1][:, 0:2, :], f1[2][:], MULT)
        nc.vector.tensor_tensor(plain[1][:, 2:4, :], early[1][:, 2:4, HALF:T], f1[3][:], MULT)
        nc.vector.tensor_tensor(plain[0][:, 0:2, :], late[0][:, 0:2, :], f0[2][:], MULT)
        nc.vector.tensor_tensor(plain[0][:, 2, :], late[0][:, 2, :], f0[3][:, 0, :], MULT)
        for c in range(2):
            block = slice(c * P, (c + 1) * P)
            nc.vector.tensor_tensor(plain[0][:, 3, block], late[0][:, 3, block], f0[3][:, 1, block], MULT)
        add_woven(z[0][:, 0:HALF], 0, P // 2)
        zf = quantise("zf", z_first, HALF)
        w2_q = [quantise("w2_0", w2_bf[0][:], P)]
        project("o0_0", zf, 0, HALF, (0,), "b4")
        add_woven(z[0][:, HALF:PASS], P // 2, P)
        w2_q.append(quantise("w2_1", w2_bf[1][:], P))
        project("o0_1", zf, 0, HALF, (1,), "b5")
        z.append(sb.tile([P, PASS], BF16, name="z1", tag="w2_0_bf", align_bytes=64))
        add_woven(z[1][:, 0:HALF], P, P + P // 2)
        z2 = quantise("z2", z[0], P)
        for m in range(N // P):
            project("o1_%d" % m, z2, HALF, P, (m,), ("b6", "b1")[m])
        add_woven(z[1][:, HALF:PASS], P + P // 2, HALF)
        z3 = (
            sb.tile([P, P], U32, name="z3_codes", align_bytes=64),
            sb.tile([P, P], U8, name="z3_scales", align_bytes=64),
        )
        for u in range(2):
            columns = slice(u * P // 2, (u + 1) * P // 2)
            quantise_into(z3[0][:, columns], z3[1][:, columns], z[1][:, u * HALF : (u + 1) * HALF])
        for m in range(N // P):
            project("o2_%d" % m, z3, HALF + P, P, (m,), ("b7", "b0")[m])
